import numpy as np
import ml_dtypes


def mxq(x, axis, fmt="e4m3"):
    dtype, down = {"e4m3": (ml_dtypes.float8_e4m3fn, 7), "e5m2": (ml_dtypes.float8_e5m2, 14)}[fmt]
    v = np.moveaxis(np.asarray(x, np.float32).astype(ml_dtypes.bfloat16).astype(np.float64), axis, -1)
    blocks = v.reshape(v.shape[:-1] + (-1, 32))
    amax = np.abs(blocks).max(-1, keepdims=True)
    byte = np.maximum(np.where(amax > 0, np.frexp(amax)[1] - 1 + 127, 0) - down, 1)
    scale = np.exp2(byte - 127.0)
    codes = (blocks / scale).astype(np.float32).astype(dtype).astype(np.float64)
    return np.moveaxis((codes * scale).reshape(v.shape), -1, axis)


WIDE = False


def mx_kscale(k):
    if not WIDE:
        return np.ones(k)
    levels = np.array([10, -10, 5, -5, 0])
    if k % 512:
        return np.exp2(np.random.permutation(np.resize(levels, k // 32))).repeat(32)
    a = np.empty((k // 512, 16))
    for p in range(k // 512):
        a[p, :8] = np.random.permutation(np.resize(levels, 8))
        for g in range(8):
            far = levels[np.abs(levels - a[p, g]) >= 10]
            a[p, g + 8] = far[np.random.randint(len(far))]
    return np.exp2(a.ravel()).repeat(32)


def f64(x):
    return np.asarray(x).astype(np.float64)


def striped(idx):
    return np.tile(idx.reshape(-1, 16).T, (8, 1)).astype(np.uint16)


def unstriped(offs):
    return offs[:16].T.reshape(-1).astype(np.int64)


def pack_weight(w):
    k, n = w.shape
    w = f64(np.asarray(w, np.float32).astype(ml_dtypes.bfloat16)).reshape(k // 32, 32, n)
    amax = np.abs(w).max(1)
    byte = np.clip(np.where(amax > 0, np.frexp(amax)[1] - 1 + 127 - 7, 1), 1, 254)
    scaled = (w * np.exp2(127.0 - byte)[:, None, :]).reshape(k, n).astype(np.float32)
    words = np.ascontiguousarray(scaled.reshape(k // 512, 128, 4, n).transpose(0, 1, 3, 2)).astype(ml_dtypes.float8_e4m3fn).view(np.uint8)
    return words, np.ascontiguousarray(byte.astype(np.uint8).reshape(k // 512, 16, n))


def unpack_weight(words, scales):
    g, p, n, _ = words.shape
    vals = np.ascontiguousarray(words).view(ml_dtypes.float8_e4m3fn).astype(np.float64) * np.repeat(np.exp2(scales.astype(np.float64) - 127.0), 8, axis=1)[..., None]
    return vals.transpose(0, 1, 3, 2).reshape(g * 512, n)


def relu(v):
    return np.maximum(v, 0.0)


K, T, S, H, N, U, V = 512, 2048, 1024, 512, 128, 1024, 512


def setup_inputs():
    n = np.random.standard_normal
    s = mx_kscale(K)[:, None]
    u = mx_kscale(H)
    packed_xT = pack_weight(n((K, T)) * s)
    return {
        "x_words": packed_xT[0],
        "x_scales": packed_xT[1],
        "w1": (n((K, H)) / np.sqrt(K) / s * u).astype(np.float32),
        "w2": (n((K, H)) / np.sqrt(K) / s * u).astype(np.float32),
        "w3": (n((H, N)) / np.sqrt(H) / u[:, None]).astype(np.float32),
        "offs": striped(np.random.permutation(T)[:S]),
        "near": striped(np.random.permutation(U)[:V]),
        "far": striped(np.random.permutation(U)[:V]),
    }


def reference(x_words, x_scales, w1, w2, w3, offs, near, far):
    xq = unpack_weight(x_words, x_scales)[:, unstriped(offs)]
    a = np.zeros((H, S))
    a[:, unstriped(near)] = relu(mxq(f64(w1), 0, "e4m3").T @ xq[:, :V])
    e = np.zeros((H, S))
    e[:, unstriped(far)] = relu(mxq(f64(w2), 0, "e4m3").T @ xq[:, V:2 * V])
    z = np.maximum(a, e)
    return mxq(f64(w3), 0, "e4m3").T @ mxq(z, 0, "e4m3")

@@ -1,0 +1,200 @@
+from contextlib import ExitStack
+
+import concourse.mybir as mybir
+
+K, T, S, H, N, V = 512, 2048, 1024, 512, 128, 512
+FLOPS = 2 * K * H * S + 2 * H * N * S
+
+F32 = mybir.dt.float32
+BF16 = mybir.dt.bfloat16
+I32 = mybir.dt.int32
+U32 = mybir.dt.uint32
+U16 = mybir.dt.uint16
+U8 = mybir.dt.uint8
+FP8X4 = mybir.dt.float8_e4m3fn_x4
+RELU = mybir.ActivationFunctionType.Relu
+MAX = mybir.AluOpType.max
+
+P = 128
+PACK = 4
+CHUNKS = (128, 256, 256, 256, 128)
+
+
+def tile_picked_bev_max_p_kernel(
+    tc, x_words, x_scales, w1, w2, w3, offs, near, far, out
+):
+    nc = tc.nc
+    with ExitStack() as ctx:
+        keep = ctx.enter_context(tc.tile_pool(name="keep", bufs=1))
+        psum = ctx.enter_context(tc.psum_pool(name="psum", bufs=4))
+
+        def sb(shape, dtype, name, tag=None):
+            return keep.tile(shape, dtype, name=name, tag=tag or name, align_bytes=64)
+
+        offs_sb = sb([P, S // 16], U16, "offs_sb")
+        near_sb = sb([P, V // 16], U16, "near_sb")
+        far_sb = sb([P, V // 16], U16, "far_sb")
+        store_scales = sb([P, T], U8, "store_scales")
+        store_words = sb([P, T], I32, "store_words")
+
+        nc.vector.memset(store_scales[:, : T // 2].bitcast(I32), 0)
+        nc.gpsimd.memset(store_scales[:, T // 2 :].bitcast(I32), 0)
+        nc.sync.dma_start(offs_sb[:], offs)
+        nc.sync.dma_start(near_sb[:], near)
+        nc.sync.dma_start(far_sb[:], far)
+        for q in range(4):
+            nc.sync.dma_start(
+                store_scales[32 * q : 32 * q + 4, :].bitcast(I32),
+                x_scales[0, 4 * q : 4 * q + 4, :].bitcast(I32),
+            )
+
+        def load_weight(w, name):
+            raw = sb([P, PACK, H], F32, name + "_raw")
+            nc.sync.dma_start(raw[:], w.rearrange("(p j) c -> p j c", j=PACK))
+            return raw
+
+        w1_raw = load_weight(w1, "w1")
+        nc.sync.dma_start(store_words[:], x_words[0].rearrange("p c r -> p (c r)").bitcast(I32))
+        w2_raw = load_weight(w2, "w2")
+
+        tiles = [sb([P, S], F32, "map%d" % b) for b in range(3)]
+        for tile in tiles:
+            nc.vector.memset(tile[:], 0.0)
+        maps = {(0, n): tiles[n == 1] for n in range(PACK)}
+        maps.update({(1, n): tiles[2] for n in range(PACK)})
+
+        picked_scales = sb([P, S], U8, "picked_scales")
+        nc.vector.tensor_copy(picked_scales[:], store_scales[:].indirect(offs_sb[:]))
+
+        def deal(copy, grouped, raw, t0, t1):
+            copy(
+                grouped[:].rearrange("p t m j -> p m j t"),
+                raw[:].rearrange("p j (m t) -> p m j t", t=PACK)[:, :, :, t0:t1],
+            )
+
+        def quantize(grouped_flat, width, name, tag=None):
+            codes = sb([P, width], U32, name + "_codes", tag)
+            scales = sb([P, width], U8, name + "_scales")
+            nc.vector.quantize_mx(out=codes[:].bitcast(FP8X4), scales=scales[:], in_=grouped_flat)
+            return codes, scales
+
+        w1_low = sb([P, 2, P, PACK], BF16, "w1_low")
+        w1_high = sb([P, 2, P, PACK], BF16, "w1_high")
+        deal(nc.vector.tensor_copy, w1_low, w1_raw, 0, 2)
+        deal(nc.scalar.copy, w1_high, w1_raw, 2, 4)
+        low = quantize(w1_low[:].rearrange("p t m j -> p (t m j)"), 2 * P, "w1_low", "shared")
+        high = quantize(w1_high[:].rearrange("p t m j -> p (t m j)"), 2 * P, "w1_high")
+        w1_q = {0: low + (0,), 1: low + (P,), 2: high + (0,), 3: high + (P,)}
+
+        picked_words = []
+        for sensor in range(2):
+            pw = sb([P, V], U32, "picked_words%d" % sensor)
+            cols = slice(sensor * V // 16, (sensor + 1) * V // 16)
+            nc.vector.tensor_copy(pw[:], store_words[:].bitcast(U32).indirect(offs_sb[:, cols]))
+            picked_words.append(pw)
+
+        def layer(sensor, wq, t):
+            acc = psum.tile([P, V], F32, name="acc")
+            codes, scales, col = wq[t]
+            nc.tensor.matmul_mx(
+                out=acc[:],
+                lhsT=codes[:, col : col + P].bitcast(FP8X4),
+                lhsT_scale=scales[:, col : col + P],
+                rhs=picked_words[sensor][:].bitcast(FP8X4),
+                rhs_scale=picked_scales[:, sensor * V : (sensor + 1) * V],
+                start=True,
+                stop=True,
+            )
+            res = sb([P, V], F32, "res%d_%d" % (sensor, t), "w2_raw" if (sensor, t) == (0, 1) else None)
+            nc.scalar.activation(res[:], acc[:], RELU)
+            return res
+
+        order = (0, 1, 2, 3)
+        res = {}
+        res[0, order[0]] = layer(0, w1_q, order[0])
+        w2_grouped = sb([P, PACK, P, PACK], BF16, "w2_grouped", "shared")
+        nc.scalar.copy(
+            w2_grouped[:].rearrange("p t m j -> p m t j"), w2_raw[:].rearrange("p j (m t) -> p m t j", t=PACK)
+        )
+        res[0, order[1]] = layer(0, w1_q, order[1])
+
+        lists = (near_sb, far_sb)
+
+        def scatter(sensor, n):
+            nc.vector.tensor_copy(maps[sensor, n][:].indirect(lists[sensor][:]), res[sensor, order[n]][:])
+
+        scatter(0, 0)
+        w2_all = quantize(w2_grouped[:].rearrange("p t m j -> p (t m j)"), H, "w2")
+        w2_q = {t: w2_all + (t * P,) for t in range(PACK)}
+        for t in order[:2]:
+            res[1, t] = layer(1, w2_q, t)
+        for t in order[2:]:
+            res[0, t] = layer(0, w1_q, t)
+            res[1, t] = layer(1, w2_q, t)
+        w3_raw = sb([P, PACK, N], F32, "w3_raw", "w1_high")
+        nc.sync.dma_start(w3_raw[:], w3.rearrange("(p j) c -> p j c", j=PACK))
+        w3_grouped = sb([P, N, PACK], BF16, "w3_grouped")
+        nc.scalar.copy(
+            w3_grouped[:].rearrange("p c (a b) -> p c a b", b=2), w3_raw[:].rearrange("p (b a) c -> p c a b", a=2)
+        )
+
+        starts = [sum(CHUNKS[:c]) for c in range(len(CHUNKS))]
+        pairs = [sb([P, 2, w, 2], BF16, "pairs%d" % c) for c, w in enumerate(CHUNKS)]
+        planes = sb([P, 2, S], BF16, "planes")
+
+        def join(n, dst, cols):
+            nc.vector.tensor_tensor(dst, maps[0, n][:, cols], maps[1, n][:, cols], MAX)
+
+        everything = slice(0, S)
+        scatter(0, 1)
+        scatter(1, 0)
+        w3_q = quantize(w3_grouped[:].rearrange("p c j -> p (c j)"), N, "w3")
+        join(0, planes[:, 0, :], everything)
+        scatter(1, 1)
+        join(1, planes[:, 1, :], everything)
+        for c, w in enumerate(CHUNKS):
+            nc.scalar.copy(pairs[c][:, 1, :, 0], planes[:, 1, starts[c] : starts[c] + w])
+        scatter(0, 2)
+        scatter(1, 2)
+        join(2, planes[:, 1, :], everything)
+        scatter(0, 3)
+        for c, w in enumerate(CHUNKS):
+            nc.scalar.copy(
+                pairs[c][:, 0, :, :], planes[:, :, starts[c] : starts[c] + w].rearrange("p e r -> p r e")
+            )
+        scatter(1, 3)
+
+        grouped = [sb([P, w, 2], U32, "z_grouped%d" % c) for c, w in enumerate(CHUNKS)]
+
+        def last_plane(c):
+            join(3, pairs[c][:, 1, :, 1], slice(starts[c], starts[c] + CHUNKS[c]))
+            words = pairs[c][:].rearrange("p h r e -> p h (r e)").bitcast(U32)
+            nc.scalar.copy(grouped[c][:], words.rearrange("p h r -> p r h"))
+
+        def finish(c):
+            w = CHUNKS[c]
+            zq = quantize(grouped[c][:].rearrange("p r h -> p (r h)").bitcast(BF16), w, "z%d" % c)
+            acc = psum.tile([P, w], F32, name="acc_out")
+            nc.tensor.matmul_mx(
+                out=acc[:],
+                lhsT=w3_q[0][:].bitcast(FP8X4),
+                lhsT_scale=w3_q[1][:],
+                rhs=zq[0][:].bitcast(FP8X4),
+                rhs_scale=zq[1][:],
+                start=True,
+                stop=True,
+            )
+            return acc
+
+        def store(c, acc, copy):
+            w = CHUNKS[c]
+            staged = sb([P, w], F32, "staged%d" % c)
+            copy(staged[:], acc[:])
+            nc.sync.dma_start(out[:, starts[c] : starts[c] + w], staged[:])
+
+        n_chunks = len(CHUNKS)
+        for c in range(n_chunks):
+            last_plane(c)
+        accs = [finish(c) for c in range(n_chunks)]
+        for c in range(n_chunks):
+            store(c, accs[c], nc.vector.tensor_copy if c % 2 == 0 else nc.scalar.copy)

@@ -14,9 +14,14 @@ U8 = mybir.dt.uint8
 FP8X4 = mybir.dt.float8_e4m3fn_x4
 RELU = mybir.ActivationFunctionType.Relu
 MAX = mybir.AluOpType.max
+ADD = mybir.AluOpType.add
+MULT = mybir.AluOpType.mult
+SUBTRACT = mybir.AluOpType.subtract
 
 P = 128
 PACK = 4
+BLOCK = 128
+SPLIT = 384
 CHUNKS = (128, 256, 256, 256, 128)
 
 
@@ -57,11 +62,11 @@ def tile_picked_bev_max_p_kernel(
         nc.sync.dma_start(store_words[:], x_words[0].rearrange("p c r -> p (c r)").bitcast(I32))
         w2_raw = load_weight(w2, "w2")
 
-        tiles = [sb([P, S], F32, "map%d" % b) for b in range(3)]
-        for tile in tiles:
+        tiles = [sb([P, S], F32, "map%d" % b) for b in range(4)]
+        for tile in tiles[:3]:
             nc.vector.memset(tile[:], 0.0)
-        maps = {(0, n): tiles[n == 1] for n in range(PACK)}
-        maps.update({(1, n): tiles[2] for n in range(PACK)})
+        nc.scalar.copy(tiles[3][:], tiles[0][:])
+        maps = {(sensor, n): tiles[2 * sensor + n % 2] for sensor in range(2) for n in range(PACK)}
 
         picked_scales = sb([P, S], U8, "picked_scales")
         nc.vector.tensor_copy(picked_scales[:], store_scales[:].indirect(offs_sb[:]))
@@ -82,7 +87,7 @@ def tile_picked_bev_max_p_kernel(
         w1_high = sb([P, 2, P, PACK], BF16, "w1_high")
         deal(nc.vector.tensor_copy, w1_low, w1_raw, 0, 2)
         deal(nc.scalar.copy, w1_high, w1_raw, 2, 4)
-        low = quantize(w1_low[:].rearrange("p t m j -> p (t m j)"), 2 * P, "w1_low", "shared")
+        low = quantize(w1_low[:].rearrange("p t m j -> p (t m j)"), 2 * P, "w1_low")
         high = quantize(w1_high[:].rearrange("p t m j -> p (t m j)"), 2 * P, "w1_high")
         w1_q = {0: low + (0,), 1: low + (P,), 2: high + (0,), 3: high + (P,)}
 
@@ -93,8 +98,8 @@ def tile_picked_bev_max_p_kernel(
             nc.vector.tensor_copy(pw[:], store_words[:].bitcast(U32).indirect(offs_sb[:, cols]))
             picked_words.append(pw)
 
-        def layer(sensor, wq, t):
-            acc = psum.tile([P, V], F32, name="acc")
+        def product(sensor, wq, t, bank):
+            acc = psum.tile([P, V], F32, name="acc", tag=bank, bufs=1)
             codes, scales, col = wq[t]
             nc.tensor.matmul_mx(
                 out=acc[:],
@@ -105,71 +110,80 @@ def tile_picked_bev_max_p_kernel(
                 start=True,
                 stop=True,
             )
-            res = sb([P, V], F32, "res%d_%d" % (sensor, t), "w2_raw" if (sensor, t) == (0, 1) else None)
-            nc.scalar.activation(res[:], acc[:], RELU)
-            return res
+            return acc
 
-        order = (0, 1, 2, 3)
-        res = {}
-        res[0, order[0]] = layer(0, w1_q, order[0])
-        w2_grouped = sb([P, PACK, P, PACK], BF16, "w2_grouped", "shared")
-        nc.scalar.copy(
-            w2_grouped[:].rearrange("p t m j -> p m t j"), w2_raw[:].rearrange("p j (m t) -> p m t j", t=PACK)
-        )
-        res[0, order[1]] = layer(0, w1_q, order[1])
+        def rectify(acc, name, v0, v1, tag=None):
+            res = sb([P, v1 - v0], F32, name, tag)
+            nc.scalar.activation(res[:], acc[:, v0:v1], RELU)
+            return res
 
         lists = (near_sb, far_sb)
 
-        def scatter(sensor, n):
-            nc.vector.tensor_copy(maps[sensor, n][:].indirect(lists[sensor][:]), res[sensor, order[n]][:])
+        def scatter(sensor, t, res, v0, v1):
+            nc.vector.tensor_copy(maps[sensor, t][:].indirect(lists[sensor][:, v0 // 16 : v1 // 16]), res[:])
 
-        scatter(0, 0)
-        w2_all = quantize(w2_grouped[:].rearrange("p t m j -> p (t m j)"), H, "w2")
-        w2_q = {t: w2_all + (t * P,) for t in range(PACK)}
-        for t in order[:2]:
-            res[1, t] = layer(1, w2_q, t)
-        for t in order[2:]:
-            res[0, t] = layer(0, w1_q, t)
-            res[1, t] = layer(1, w2_q, t)
+        def gpsimd_cast(dst, src):
+            nc.gpsimd.tensor_scalar(dst, src, 1.0, 0.0, MULT, ADD)
+
+        first = product(0, w1_q, 0, "first")
+        scatter(0, 0, rectify(first, "res_head", 0, SPLIT), 0, SPLIT)
+        w2_low = sb([P, 2, P, PACK], BF16, "w2_low")
+        w2_high = sb([P, 2, P, PACK], BF16, "w2_high")
+        deal(nc.scalar.copy, w2_low, w2_raw, 0, 2)
+        deal(nc.scalar.copy, w2_high, w2_raw, 2, 4)
+        low = quantize(w2_low[:].rearrange("p t m j -> p (t m j)"), 2 * P, "w2_low")
+        high = quantize(w2_high[:].rearrange("p t m j -> p (t m j)"), 2 * P, "w2_high")
+        w2_q = {0: low + (0,), 1: low + (P,), 2: high + (0,), 3: high + (P,)}
+        scatter(0, 0, rectify(first, "res_rest", SPLIT, V, "w2_raw"), SPLIT, V)
+
+        res = {}
+        for t in range(PACK):
+            for sensor, wq in enumerate((w1_q, w2_q)):
+                if (sensor, t) != (0, 0):
+                    res[sensor, t] = rectify(product(sensor, wq, t, "chain"), "res%d_%d" % (sensor, t), 0, V, "w2_high" if t == 0 else None)
+
         w3_raw = sb([P, PACK, N], F32, "w3_raw", "w1_high")
         nc.sync.dma_start(w3_raw[:], w3.rearrange("(p j) c -> p j c", j=PACK))
-        w3_grouped = sb([P, N, PACK], BF16, "w3_grouped")
-        nc.scalar.copy(
+        w3_grouped = sb([P, N, PACK], BF16, "w3_grouped", "w2_raw")
+        gpsimd_cast(
             w3_grouped[:].rearrange("p c (a b) -> p c a b", b=2), w3_raw[:].rearrange("p (b a) c -> p c a b", a=2)
         )
 
         starts = [sum(CHUNKS[:c]) for c in range(len(CHUNKS))]
-        pairs = [sb([P, 2, w, 2], BF16, "pairs%d" % c) for c, w in enumerate(CHUNKS)]
-        planes = sb([P, 2, S], BF16, "planes")
+        pairs = sb([P, PACK * S], BF16, "pairs")
+        pair_view = pairs[:].rearrange("p (b h r e) -> p b h r e", h=2, r=BLOCK, e=2)
 
-        def join(n, dst, cols):
-            nc.vector.tensor_tensor(dst, maps[0, n][:, cols], maps[1, n][:, cols], MAX)
+        def slot(t, r0, r1):
+            return pair_view[:, r0 // BLOCK : r1 // BLOCK, t % 2, :, t // 2]
 
-        everything = slice(0, S)
-        scatter(0, 1)
-        scatter(1, 0)
+        def cells(tile, r0, r1):
+            return tile[:, r0:r1].rearrange("p (b r) -> p b r", r=BLOCK)
+
+        def join_aside(t):
+            halves = ((0, S // 2), (S // 2, S))
+            excess = []
+            for h, (r0, r1) in enumerate(halves):
+                gap = sb([P, S // 2], F32, "gap%d_%d" % (t, h))
+                excess.append(sb([P, S // 2], F32, "excess%d_%d" % (t, h)))
+                nc.gpsimd.tensor_tensor(gap[:], maps[0, t][:, r0:r1], maps[1, t][:, r0:r1], SUBTRACT)
+                nc.scalar.activation(excess[h][:], gap[:], RELU)
+            for h, (r0, r1) in enumerate(halves):
+                nc.gpsimd.tensor_tensor(slot(t, r0, r1), cells(excess[h], 0, S // 2), cells(maps[1, t], r0, r1), ADD)
+
+        scatter(1, 0, res[1, 0], 0, V)
         w3_q = quantize(w3_grouped[:].rearrange("p c j -> p (c j)"), N, "w3")
-        join(0, planes[:, 0, :], everything)
-        scatter(1, 1)
-        join(1, planes[:, 1, :], everything)
-        for c, w in enumerate(CHUNKS):
-            nc.scalar.copy(pairs[c][:, 1, :, 0], planes[:, 1, starts[c] : starts[c] + w])
-        scatter(0, 2)
-        scatter(1, 2)
-        join(2, planes[:, 1, :], everything)
-        scatter(0, 3)
-        for c, w in enumerate(CHUNKS):
-            nc.scalar.copy(
-                pairs[c][:, 0, :, :], planes[:, :, starts[c] : starts[c] + w].rearrange("p e r -> p r e")
-            )
-        scatter(1, 3)
+        for t in range(1, PACK):
+            join_aside(t - 1)
+            scatter(0, t, res[0, t], 0, V)
+            scatter(1, t, res[1, t], 0, V)
 
         grouped = [sb([P, w, 2], U32, "z_grouped%d" % c) for c, w in enumerate(CHUNKS)]
 
         def last_plane(c):
-            join(3, pairs[c][:, 1, :, 1], slice(starts[c], starts[c] + CHUNKS[c]))
-            words = pairs[c][:].rearrange("p h r e -> p h (r e)").bitcast(U32)
-            nc.scalar.copy(grouped[c][:], words.rearrange("p h r -> p r h"))
+            r0, r1 = starts[c], starts[c] + CHUNKS[c]
+            nc.vector.tensor_tensor(slot(3, r0, r1), cells(maps[0, 3], r0, r1), cells(maps[1, 3], r0, r1), MAX)
+            words = pairs[:, PACK * r0 : PACK * r1].bitcast(U32).rearrange("p (b h r) -> p b r h", h=2, r=BLOCK)
+            nc.scalar.copy(grouped[c][:].rearrange("p (b r) h -> p b r h", r=BLOCK), words)
 
         def finish(c):
             w = CHUNKS[c]
@@ -197,4 +211,4 @@ def tile_picked_bev_max_p_kernel(
             last_plane(c)
         accs = [finish(c) for c in range(n_chunks)]
         for c in range(n_chunks):
-            store(c, accs[c], nc.vector.tensor_copy if c % 2 == 0 else nc.scalar.copy)
+            store(c, accs[c], nc.vector.tensor_copy if c == n_chunks - 1 else nc.scalar.copy)

@@ -42,8 +42,7 @@ def tile_picked_bev_max_p_kernel(
         store_scales = sb([P, T], U8, "store_scales")
         store_words = sb([P, T], I32, "store_words")
 
-        nc.vector.memset(store_scales[:, : T // 2].bitcast(I32), 0)
-        nc.gpsimd.memset(store_scales[:, T // 2 :].bitcast(I32), 0)
+        nc.vector.memset(store_scales[:].bitcast(I32), 0)
         nc.sync.dma_start(offs_sb[:], offs)
         nc.sync.dma_start(near_sb[:], near)
         nc.sync.dma_start(far_sb[:], far)

@@ -22,6 +22,7 @@ P = 128
 PACK = 4
 BLOCK = 128
 SPLIT = 384
+SHARE = 88
 CHUNKS = (128, 256, 256, 256, 128)
 
 
@@ -46,25 +47,22 @@ def tile_picked_bev_max_p_kernel(
         nc.sync.dma_start(offs_sb[:], offs)
         nc.sync.dma_start(near_sb[:], near)
         nc.sync.dma_start(far_sb[:], far)
-        for q in range(4):
-            nc.sync.dma_start(
-                store_scales[32 * q : 32 * q + 4, :].bitcast(I32),
-                x_scales[0, 4 * q : 4 * q + 4, :].bitcast(I32),
-            )
+        for r in range(4):
+            nc.sync.dma_start(store_scales[r:P:32, :].bitcast(I32), x_scales[0, r:16:4, :].bitcast(I32))
 
         def load_weight(w, name):
             raw = sb([P, PACK, H], F32, name + "_raw")
             nc.sync.dma_start(raw[:], w.rearrange("(p j) c -> p j c", j=PACK))
             return raw
 
-        w1_raw = load_weight(w1, "w1")
         nc.sync.dma_start(store_words[:], x_words[0].rearrange("p c r -> p (c r)").bitcast(I32))
+        w1_raw = load_weight(w1, "w1")
         w2_raw = load_weight(w2, "w2")
 
         tiles = [sb([P, S], F32, "map%d" % b) for b in range(4)]
-        for tile in tiles[:3]:
-            nc.vector.memset(tile[:], 0.0)
-        nc.scalar.copy(tiles[3][:], tiles[0][:])
+        for b in (0, 2):
+            nc.vector.memset(tiles[b][:], 0.0)
+            nc.scalar.copy(tiles[b + 1][:], tiles[b][:])
         maps = {(sensor, n): tiles[2 * sensor + n % 2] for sensor in range(2) for n in range(PACK)}
 
         picked_scales = sb([P, S], U8, "picked_scales")
@@ -82,33 +80,45 @@ def tile_picked_bev_max_p_kernel(
             nc.vector.quantize_mx(out=codes[:].bitcast(FP8X4), scales=scales[:], in_=grouped_flat)
             return codes, scales
 
-        w1_low = sb([P, 2, P, PACK], BF16, "w1_low")
+        def pick(name, c0, c1, tag=None):
+            pw = sb([P, c1 - c0], U32, name, tag)
+            nc.vector.tensor_copy(pw[:], store_words[:].bitcast(U32).indirect(offs_sb[:, c0 // 16 : c1 // 16]))
+            return pw
+
+        words0 = pick("words0", 0, V)
+        words1 = [pick("words1a", V, V + V // 2)]
+        w1_low = sb([P, 2 * P * PACK], BF16, "w1_low")
         w1_high = sb([P, 2, P, PACK], BF16, "w1_high")
-        deal(nc.vector.tensor_copy, w1_low, w1_raw, 0, 2)
+        low_view = w1_low[:].rearrange("p (t m j) -> p m j t", t=2, j=PACK)
+        raw_view = w1_raw[:].rearrange("p j (m t) -> p m j t", t=PACK)
+        nc.vector.tensor_copy(low_view[:, :SHARE, :, :], raw_view[:, :SHARE, :, 0:2])
+        nc.scalar.copy(low_view[:, SHARE:, :, :], raw_view[:, SHARE:, :, 0:2])
         deal(nc.scalar.copy, w1_high, w1_raw, 2, 4)
-        low = quantize(w1_low[:].rearrange("p t m j -> p (t m j)"), 2 * P, "w1_low")
+        low = quantize(w1_low[:], 2 * P, "w1_low")
+        words1.append(pick("words1b", V + V // 2, S, "w1_low"))
         high = quantize(w1_high[:].rearrange("p t m j -> p (t m j)"), 2 * P, "w1_high")
         w1_q = {0: low + (0,), 1: low + (P,), 2: high + (0,), 3: high + (P,)}
+        picked = {(0, h): words0[:, h * V // 2 : (h + 1) * V // 2] for h in range(2)}
+        for h in range(2):
+            picked[1, h] = words1[h][:]
 
-        picked_words = []
-        for sensor in range(2):
-            pw = sb([P, V], U32, "picked_words%d" % sensor)
-            cols = slice(sensor * V // 16, (sensor + 1) * V // 16)
-            nc.vector.tensor_copy(pw[:], store_words[:].bitcast(U32).indirect(offs_sb[:, cols]))
-            picked_words.append(pw)
-
-        def product(sensor, wq, t, bank):
-            acc = psum.tile([P, V], F32, name="acc", tag=bank, bufs=1)
+        def multiply(acc, sensor, wq, t, h):
             codes, scales, col = wq[t]
+            c0 = sensor * V + h * V // 2
             nc.tensor.matmul_mx(
-                out=acc[:],
+                out=acc,
                 lhsT=codes[:, col : col + P].bitcast(FP8X4),
                 lhsT_scale=scales[:, col : col + P],
-                rhs=picked_words[sensor][:].bitcast(FP8X4),
-                rhs_scale=picked_scales[:, sensor * V : (sensor + 1) * V],
+                rhs=picked[sensor, h].bitcast(FP8X4),
+                rhs_scale=picked_scales[:, c0 : c0 + V // 2],
                 start=True,
                 stop=True,
             )
+
+        def product(sensor, wq, t, bank):
+            acc = psum.tile([P, V], F32, name="acc", tag=bank, bufs=1)
+            for h in range(2):
+                multiply(acc[:, h * V // 2 : (h + 1) * V // 2], sensor, wq, t, h)
             return acc
 
         def rectify(acc, name, v0, v1, tag=None):
@@ -124,8 +134,11 @@ def tile_picked_bev_max_p_kernel(
         def gpsimd_cast(dst, src):
             nc.gpsimd.tensor_scalar(dst, src, 1.0, 0.0, MULT, ADD)
 
-        first = product(0, w1_q, 0, "first")
-        scatter(0, 0, rectify(first, "res_head", 0, SPLIT), 0, SPLIT)
+        first = [psum.tile([P, V // 2], F32, name="first%d" % h, tag="first%d" % h, bufs=1) for h in range(2)]
+        for h in range(2):
+            multiply(first[h][:], 0, w1_q, 0, h)
+        scatter(0, 0, rectify(first[0], "res_head", 0, V // 2), 0, V // 2)
+        scatter(0, 0, rectify(first[1], "res_mid", 0, SPLIT - V // 2), V // 2, SPLIT)
         w2_low = sb([P, 2, P, PACK], BF16, "w2_low")
         w2_high = sb([P, 2, P, PACK], BF16, "w2_high")
         deal(nc.scalar.copy, w2_low, w2_raw, 0, 2)
@@ -133,7 +146,7 @@ def tile_picked_bev_max_p_kernel(
         low = quantize(w2_low[:].rearrange("p t m j -> p (t m j)"), 2 * P, "w2_low")
         high = quantize(w2_high[:].rearrange("p t m j -> p (t m j)"), 2 * P, "w2_high")
         w2_q = {0: low + (0,), 1: low + (P,), 2: high + (0,), 3: high + (P,)}
-        scatter(0, 0, rectify(first, "res_rest", SPLIT, V, "w2_raw"), SPLIT, V)
+        scatter(0, 0, rectify(first[1], "res_rest", SPLIT - V // 2, V // 2, "w2_raw"), SPLIT, V)
 
         res = {}
         for t in range(PACK):

@@ -15,13 +15,12 @@ FP8X4 = mybir.dt.float8_e4m3fn_x4
 RELU = mybir.ActivationFunctionType.Relu
 MAX = mybir.AluOpType.max
 ADD = mybir.AluOpType.add
-MULT = mybir.AluOpType.mult
 SUBTRACT = mybir.AluOpType.subtract
 
 P = 128
 PACK = 4
 BLOCK = 128
-SPLIT = 384
+SPLIT = 320
 SHARE = 88
 CHUNKS = (128, 256, 256, 256, 128)
 
@@ -47,8 +46,10 @@ def tile_picked_bev_max_p_kernel(
         nc.sync.dma_start(offs_sb[:], offs)
         nc.sync.dma_start(near_sb[:], near)
         nc.sync.dma_start(far_sb[:], far)
-        for r in range(4):
-            nc.sync.dma_start(store_scales[r:P:32, :].bitcast(I32), x_scales[0, r:16:4, :].bitcast(I32))
+        for q in range(4):
+            nc.sync.dma_start(
+                store_scales[32 * q : 32 * q + 4, :].bitcast(I32), x_scales[0, 4 * q : 4 * q + 4, :].bitcast(I32)
+            )
 
         def load_weight(w, name):
             raw = sb([P, PACK, H], F32, name + "_raw")
@@ -131,14 +132,13 @@ def tile_picked_bev_max_p_kernel(
         def scatter(sensor, t, res, v0, v1):
             nc.vector.tensor_copy(maps[sensor, t][:].indirect(lists[sensor][:, v0 // 16 : v1 // 16]), res[:])
 
-        def gpsimd_cast(dst, src):
-            nc.gpsimd.tensor_scalar(dst, src, 1.0, 0.0, MULT, ADD)
-
         first = [psum.tile([P, V // 2], F32, name="first%d" % h, tag="first%d" % h, bufs=1) for h in range(2)]
         for h in range(2):
             multiply(first[h][:], 0, w1_q, 0, h)
-        scatter(0, 0, rectify(first[0], "res_head", 0, V // 2), 0, V // 2)
-        scatter(0, 0, rectify(first[1], "res_mid", 0, SPLIT - V // 2), V // 2, SPLIT)
+        head = sb([P, SPLIT], F32, "res_head")
+        nc.scalar.activation(head[:, : V // 2], first[0][:], RELU)
+        nc.scalar.activation(head[:, V // 2 :], first[1][:, : SPLIT - V // 2], RELU)
+        scatter(0, 0, head, 0, SPLIT)
         w2_low = sb([P, 2, P, PACK], BF16, "w2_low")
         w2_high = sb([P, 2, P, PACK], BF16, "w2_high")
         deal(nc.scalar.copy, w2_low, w2_raw, 0, 2)
@@ -148,18 +148,20 @@ def tile_picked_bev_max_p_kernel(
         w2_q = {0: low + (0,), 1: low + (P,), 2: high + (0,), 3: high + (P,)}
         scatter(0, 0, rectify(first[1], "res_rest", SPLIT - V // 2, V // 2, "w2_raw"), SPLIT, V)
 
+        w3_raw = sb([P, PACK, N], F32, "w3_raw")
+        nc.sync.dma_start(w3_raw[:], w3.rearrange("(p j) c -> p j c", j=PACK))
+        w3_grouped = sb([P, N, PACK], BF16, "w3_grouped")
+        nc.scalar.copy(
+            w3_grouped[:].rearrange("p c (a b) -> p c a b", b=2), w3_raw[:].rearrange("p (b a) c -> p c a b", a=2)
+        )
+
+        w3_q = quantize(w3_grouped[:].rearrange("p c j -> p (c j)"), N, "w3")
+
         res = {}
         for t in range(PACK):
             for sensor, wq in enumerate((w1_q, w2_q)):
                 if (sensor, t) != (0, 0):
                     res[sensor, t] = rectify(product(sensor, wq, t, "chain"), "res%d_%d" % (sensor, t), 0, V, "w2_high" if t == 0 else None)
-
-        w3_raw = sb([P, PACK, N], F32, "w3_raw", "w1_high")
-        nc.sync.dma_start(w3_raw[:], w3.rearrange("(p j) c -> p j c", j=PACK))
-        w3_grouped = sb([P, N, PACK], BF16, "w3_grouped", "w2_raw")
-        gpsimd_cast(
-            w3_grouped[:].rearrange("p c (a b) -> p c a b", b=2), w3_raw[:].rearrange("p (b a) c -> p c a b", a=2)
-        )
 
         starts = [sum(CHUNKS[:c]) for c in range(len(CHUNKS))]
         pairs = sb([P, PACK * S], BF16, "pairs")
@@ -183,7 +185,6 @@ def tile_picked_bev_max_p_kernel(
                 nc.gpsimd.tensor_tensor(slot(t, r0, r1), cells(excess[h], 0, S // 2), cells(maps[1, t], r0, r1), ADD)
 
         scatter(1, 0, res[1, 0], 0, V)
-        w3_q = quantize(w3_grouped[:].rearrange("p c j -> p (c j)"), N, "w3")
         for t in range(1, PACK):
             join_aside(t - 1)
             scatter(0, t, res[0, t], 0, V)

@@ -21,7 +21,8 @@ P = 128
 PACK = 4
 BLOCK = 128
 SPLIT = 320
-SHARE = 88
+SHARE = 80
+AHEAD = 512
 CHUNKS = (128, 256, 256, 256, 128)
 
 
@@ -44,8 +45,9 @@ def tile_picked_bev_max_p_kernel(
 
         nc.vector.memset(store_scales[:].bitcast(I32), 0)
         nc.sync.dma_start(offs_sb[:], offs)
+        words_in = x_words[0].rearrange("p c r -> p (c r)").bitcast(I32)
+        nc.sync.dma_start(store_words[:, :AHEAD], words_in[:, :AHEAD])
         nc.sync.dma_start(near_sb[:], near)
-        nc.sync.dma_start(far_sb[:], far)
         for q in range(4):
             nc.sync.dma_start(
                 store_scales[32 * q : 32 * q + 4, :].bitcast(I32), x_scales[0, 4 * q : 4 * q + 4, :].bitcast(I32)
@@ -56,14 +58,15 @@ def tile_picked_bev_max_p_kernel(
             nc.sync.dma_start(raw[:], w.rearrange("(p j) c -> p j c", j=PACK))
             return raw
 
-        nc.sync.dma_start(store_words[:], x_words[0].rearrange("p c r -> p (c r)").bitcast(I32))
+        nc.sync.dma_start(store_words[:, AHEAD:], words_in[:, AHEAD:])
         w1_raw = load_weight(w1, "w1")
+        nc.sync.dma_start(far_sb[:], far)
         w2_raw = load_weight(w2, "w2")
 
         tiles = [sb([P, S], F32, "map%d" % b) for b in range(4)]
-        for b in (0, 2):
-            nc.vector.memset(tiles[b][:], 0.0)
-            nc.scalar.copy(tiles[b + 1][:], tiles[b][:])
+        nc.vector.memset(tiles[0][:], 0.0)
+        for b in (2, 1, 3):
+            nc.scalar.copy(tiles[b][:], tiles[0][:])
         maps = {(sensor, n): tiles[2 * sensor + n % 2] for sensor in range(2) for n in range(PACK)}
 
         picked_scales = sb([P, S], U8, "picked_scales")
@@ -87,7 +90,6 @@ def tile_picked_bev_max_p_kernel(
             return pw
 
         words0 = pick("words0", 0, V)
-        words1 = [pick("words1a", V, V + V // 2)]
         w1_low = sb([P, 2 * P * PACK], BF16, "w1_low")
         w1_high = sb([P, 2, P, PACK], BF16, "w1_high")
         low_view = w1_low[:].rearrange("p (t m j) -> p m j t", t=2, j=PACK)
@@ -96,30 +98,25 @@ def tile_picked_bev_max_p_kernel(
         nc.scalar.copy(low_view[:, SHARE:, :, :], raw_view[:, SHARE:, :, 0:2])
         deal(nc.scalar.copy, w1_high, w1_raw, 2, 4)
         low = quantize(w1_low[:], 2 * P, "w1_low")
-        words1.append(pick("words1b", V + V // 2, S, "w1_low"))
+        words = (words0, pick("words1", V, S, "w1_low"))
         high = quantize(w1_high[:].rearrange("p t m j -> p (t m j)"), 2 * P, "w1_high")
         w1_q = {0: low + (0,), 1: low + (P,), 2: high + (0,), 3: high + (P,)}
-        picked = {(0, h): words0[:, h * V // 2 : (h + 1) * V // 2] for h in range(2)}
-        for h in range(2):
-            picked[1, h] = words1[h][:]
 
-        def multiply(acc, sensor, wq, t, h):
+        def multiply(acc, sensor, wq, t, v0, v1):
             codes, scales, col = wq[t]
-            c0 = sensor * V + h * V // 2
             nc.tensor.matmul_mx(
                 out=acc,
                 lhsT=codes[:, col : col + P].bitcast(FP8X4),
                 lhsT_scale=scales[:, col : col + P],
-                rhs=picked[sensor, h].bitcast(FP8X4),
-                rhs_scale=picked_scales[:, c0 : c0 + V // 2],
+                rhs=words[sensor][:, v0:v1].bitcast(FP8X4),
+                rhs_scale=picked_scales[:, sensor * V + v0 : sensor * V + v1],
                 start=True,
                 stop=True,
             )
 
         def product(sensor, wq, t, bank):
             acc = psum.tile([P, V], F32, name="acc", tag=bank, bufs=1)
-            for h in range(2):
-                multiply(acc[:, h * V // 2 : (h + 1) * V // 2], sensor, wq, t, h)
+            multiply(acc[:], sensor, wq, t, 0, V)
             return acc
 
         def rectify(acc, name, v0, v1, tag=None):
@@ -134,7 +131,7 @@ def tile_picked_bev_max_p_kernel(
 
         first = [psum.tile([P, V // 2], F32, name="first%d" % h, tag="first%d" % h, bufs=1) for h in range(2)]
         for h in range(2):
-            multiply(first[h][:], 0, w1_q, 0, h)
+            multiply(first[h][:], 0, w1_q, 0, h * V // 2, (h + 1) * V // 2)
         head = sb([P, SPLIT], F32, "res_head")
         nc.scalar.activation(head[:, : V // 2], first[0][:], RELU)
         nc.scalar.activation(head[:, V // 2 :], first[1][:, : SPLIT - V // 2], RELU)

@@ -24,6 +24,7 @@ SPLIT = 320
 SHARE = 80
 AHEAD = 512
 CHUNKS = (128, 256, 256, 256, 128)
+MAXIMA = (128, 256, 256, 384)
 
 
 def tile_picked_bev_max_p_kernel(
@@ -154,11 +155,14 @@ def tile_picked_bev_max_p_kernel(
 
         w3_q = quantize(w3_grouped[:].rearrange("p c j -> p (c j)"), N, "w3")
 
-        res = {}
-        for t in range(PACK):
+        res = {(1, 0): sb([P, V], F32, "res1_0", "w2_high")}
+        for bank, v0 in (("first0", 0), ("chain", V // 2)):
+            acc = psum.tile([P, V // 2], F32, name="second", tag=bank, bufs=1)
+            multiply(acc[:], 1, w2_q, 0, v0, v0 + V // 2)
+            nc.scalar.activation(res[1, 0][:, v0 : v0 + V // 2], acc[:], RELU)
+        for t in range(1, PACK):
             for sensor, wq in enumerate((w1_q, w2_q)):
-                if (sensor, t) != (0, 0):
-                    res[sensor, t] = rectify(product(sensor, wq, t, "chain"), "res%d_%d" % (sensor, t), 0, V, "w2_high" if t == 0 else None)
+                res[sensor, t] = rectify(product(sensor, wq, t, "chain"), "res%d_%d" % (sensor, t), 0, V)
 
         starts = [sum(CHUNKS[:c]) for c in range(len(CHUNKS))]
         pairs = sb([P, PACK * S], BF16, "pairs")
@@ -189,9 +193,11 @@ def tile_picked_bev_max_p_kernel(
 
         grouped = [sb([P, w, 2], U32, "z_grouped%d" % c) for c, w in enumerate(CHUNKS)]
 
-        def last_plane(c):
-            r0, r1 = starts[c], starts[c] + CHUNKS[c]
+        def last_plane(r0, r1):
             nc.vector.tensor_tensor(slot(3, r0, r1), cells(maps[0, 3], r0, r1), cells(maps[1, 3], r0, r1), MAX)
+
+        def weave(c):
+            r0, r1 = starts[c], starts[c] + CHUNKS[c]
             words = pairs[:, PACK * r0 : PACK * r1].bitcast(U32).rearrange("p (b h r) -> p b r h", h=2, r=BLOCK)
             nc.scalar.copy(grouped[c][:].rearrange("p (b r) h -> p b r h", r=BLOCK), words)
 
@@ -217,8 +223,10 @@ def tile_picked_bev_max_p_kernel(
             nc.sync.dma_start(out[:, starts[c] : starts[c] + w], staged[:])
 
         n_chunks = len(CHUNKS)
+        for m in range(len(MAXIMA)):
+            last_plane(sum(MAXIMA[:m]), sum(MAXIMA[: m + 1]))
         for c in range(n_chunks):
-            last_plane(c)
+            weave(c)
         accs = [finish(c) for c in range(n_chunks)]
         for c in range(n_chunks):
-            store(c, accs[c], nc.vector.tensor_copy if c == n_chunks - 1 else nc.scalar.copy)
+            store(c, accs[c], nc.vector.tensor_copy if c >= n_chunks - 1 else nc.scalar.copy)

@@ -20,8 +20,7 @@ SUBTRACT = mybir.AluOpType.subtract
 P = 128
 PACK = 4
 BLOCK = 128
-SPLIT = 320
-SHARE = 80
+SHARE = 8
 AHEAD = 512
 CHUNKS = (128, 256, 256, 256, 128)
 MAXIMA = (128, 256, 256, 384)
@@ -33,6 +32,7 @@ def tile_picked_bev_max_p_kernel(
     nc = tc.nc
     with ExitStack() as ctx:
         keep = ctx.enter_context(tc.tile_pool(name="keep", bufs=1))
+        reuse = ctx.enter_context(tc.tile_pool(name="reuse", bufs=1))
         psum = ctx.enter_context(tc.psum_pool(name="psum", bufs=4))
 
         def sb(shape, dtype, name, tag=None):
@@ -63,6 +63,10 @@ def tile_picked_bev_max_p_kernel(
         w1_raw = load_weight(w1, "w1")
         nc.sync.dma_start(far_sb[:], far)
         w2_raw = load_weight(w2, "w2")
+        w3_raw = reuse.tile([P, PACK, N], F32, name="w3_raw", offset=0, align_bytes=64)
+        w3_rows = w3.rearrange("(b t s) c -> t b s c", t=PACK, s=8)
+        for t in range(PACK):
+            nc.sync.dma_start(w3_raw[:, t, :], w3_rows[t])
 
         tiles = [sb([P, S], F32, "map%d" % b) for b in range(4)]
         nc.vector.memset(tiles[0][:], 0.0)
@@ -73,11 +77,10 @@ def tile_picked_bev_max_p_kernel(
         picked_scales = sb([P, S], U8, "picked_scales")
         nc.vector.tensor_copy(picked_scales[:], store_scales[:].indirect(offs_sb[:]))
 
-        def deal(copy, grouped, raw, t0, t1):
-            copy(
-                grouped[:].rearrange("p t m j -> p m j t"),
-                raw[:].rearrange("p j (m t) -> p m j t", t=PACK)[:, :, :, t0:t1],
-            )
+        def deal(copy, grouped, place, raw, t, b0=0, b1=16):
+            plane = grouped[:, place * H : (place + 1) * H].rearrange("p (b s j) -> p b s j", s=8, j=PACK)
+            rows = raw[:].rearrange("p j (b t s) -> p t b s j", t=PACK, s=8)
+            copy(plane[:, b0:b1], rows[:, t, b0:b1])
 
         def quantize(grouped_flat, width, name, tag=None):
             codes = sb([P, width], U32, name + "_codes", tag)
@@ -90,21 +93,29 @@ def tile_picked_bev_max_p_kernel(
             nc.vector.tensor_copy(pw[:], store_words[:].bitcast(U32).indirect(offs_sb[:, c0 // 16 : c1 // 16]))
             return pw
 
-        words0 = pick("words0", 0, V)
-        w1_low = sb([P, 2 * P * PACK], BF16, "w1_low")
-        w1_high = sb([P, 2, P, PACK], BF16, "w1_high")
-        low_view = w1_low[:].rearrange("p (t m j) -> p m j t", t=2, j=PACK)
-        raw_view = w1_raw[:].rearrange("p j (m t) -> p m j t", t=PACK)
-        nc.vector.tensor_copy(low_view[:, :SHARE, :, :], raw_view[:, :SHARE, :, 0:2])
-        nc.scalar.copy(low_view[:, SHARE:, :, :], raw_view[:, SHARE:, :, 0:2])
-        deal(nc.scalar.copy, w1_high, w1_raw, 2, 4)
-        low = quantize(w1_low[:], 2 * P, "w1_low")
-        words = (words0, pick("words1", V, S, "w1_low"))
-        high = quantize(w1_high[:].rearrange("p t m j -> p (t m j)"), 2 * P, "w1_high")
-        w1_q = {0: low + (0,), 1: low + (P,), 2: high + (0,), 3: high + (P,)}
+        raws = (w1_raw, w2_raw)
+        quantised = {}
 
-        def multiply(acc, sensor, wq, t, v0, v1):
-            codes, scales, col = wq[t]
+        def prepare(name, planes):
+            grouped = sb([P, len(planes) * H], BF16, name)
+            for place, (sensor, t) in enumerate(planes):
+                deal(nc.scalar.copy, grouped, place, raws[sensor], t)
+            return grouped
+
+        def settle(name, grouped, planes):
+            made = quantize(grouped[:], len(planes) * P, name)
+            for place, key in enumerate(planes):
+                quantised[key] = made + (place * P,)
+
+        words0 = pick("words0", 0, V)
+        lead = sb([P, 2 * H], BF16, "lead")
+        deal(nc.vector.tensor_copy, lead, 0, w1_raw, 0, 0, SHARE)
+        deal(nc.scalar.copy, lead, 0, w1_raw, 0, SHARE, 16)
+        quantised[0, 0] = quantize(lead[:, :H], P, "lead") + (0,)
+        words = (words0, pick("words1", V, S, "lead"))
+
+        def multiply(acc, sensor, t, v0, v1):
+            codes, scales, col = quantised[sensor, t]
             nc.tensor.matmul_mx(
                 out=acc,
                 lhsT=codes[:, col : col + P].bitcast(FP8X4),
@@ -115,54 +126,54 @@ def tile_picked_bev_max_p_kernel(
                 stop=True,
             )
 
-        def product(sensor, wq, t, bank):
-            acc = psum.tile([P, V], F32, name="acc", tag=bank, bufs=1)
-            multiply(acc[:], sensor, wq, t, 0, V)
-            return acc
-
-        def rectify(acc, name, v0, v1, tag=None):
-            res = sb([P, v1 - v0], F32, name, tag)
-            nc.scalar.activation(res[:], acc[:, v0:v1], RELU)
-            return res
-
         lists = (near_sb, far_sb)
 
         def scatter(sensor, t, res, v0, v1):
-            nc.vector.tensor_copy(maps[sensor, t][:].indirect(lists[sensor][:, v0 // 16 : v1 // 16]), res[:])
+            nc.vector.tensor_copy(maps[sensor, t][:].indirect(lists[sensor][:, v0 // 16 : v1 // 16]), res)
 
-        first = [psum.tile([P, V // 2], F32, name="first%d" % h, tag="first%d" % h, bufs=1) for h in range(2)]
+        half = V // 2
+        first = [psum.tile([P, half], F32, name="first%d" % h, tag="first%d" % h, bufs=1) for h in range(2)]
         for h in range(2):
-            multiply(first[h][:], 0, w1_q, 0, h * V // 2, (h + 1) * V // 2)
-        head = sb([P, SPLIT], F32, "res_head")
-        nc.scalar.activation(head[:, : V // 2], first[0][:], RELU)
-        nc.scalar.activation(head[:, V // 2 :], first[1][:, : SPLIT - V // 2], RELU)
-        scatter(0, 0, head, 0, SPLIT)
-        w2_low = sb([P, 2, P, PACK], BF16, "w2_low")
-        w2_high = sb([P, 2, P, PACK], BF16, "w2_high")
-        deal(nc.scalar.copy, w2_low, w2_raw, 0, 2)
-        deal(nc.scalar.copy, w2_high, w2_raw, 2, 4)
-        low = quantize(w2_low[:].rearrange("p t m j -> p (t m j)"), 2 * P, "w2_low")
-        high = quantize(w2_high[:].rearrange("p t m j -> p (t m j)"), 2 * P, "w2_high")
-        w2_q = {0: low + (0,), 1: low + (P,), 2: high + (0,), 3: high + (P,)}
-        scatter(0, 0, rectify(first[1], "res_rest", SPLIT - V // 2, V // 2, "w2_raw"), SPLIT, V)
+            multiply(first[h][:], 0, 0, h * half, (h + 1) * half)
+        second = prepare("second", [(0, 1)])
+        head = sb([P, half], F32, "res_head")
+        nc.scalar.activation(head[:], first[0][:], RELU)
+        settle("second", second, [(0, 1)])
+        scatter(0, 0, head[:], 0, half)
 
-        w3_raw = sb([P, PACK, N], F32, "w3_raw")
-        nc.sync.dma_start(w3_raw[:], w3.rearrange("(p j) c -> p j c", j=PACK))
-        w3_grouped = sb([P, N, PACK], BF16, "w3_grouped")
+        third = prepare("third", [(1, 0)])
+        w3_grouped = sb([P, N * PACK], BF16, "w3_grouped")
         nc.scalar.copy(
-            w3_grouped[:].rearrange("p c (a b) -> p c a b", b=2), w3_raw[:].rearrange("p (b a) c -> p c a b", a=2)
+            w3_grouped[:].rearrange("p (c a b) -> p c a b", a=2, b=2),
+            w3_raw[:].rearrange("p (b a) c -> p c a b", a=2),
         )
+        rest = reuse.tile([P, half], F32, name="res_rest", offset=0, align_bytes=64)
+        nc.scalar.activation(rest[:], first[1][:], RELU)
+        settle("third", third, [(1, 0)])
+        settle("w3", w3_grouped, ["w3"])
+        scatter(0, 0, rest[:], half, V)
 
-        w3_q = quantize(w3_grouped[:].rearrange("p c j -> p (c j)"), N, "w3")
+        fourth = reuse.tile([P, H], BF16, name="fourth", offset=4 * half, align_bytes=64)
+        deal(nc.scalar.copy, fourth, 0, w2_raw, 1)
+        res = {}
 
-        res = {(1, 0): sb([P, V], F32, "res1_0", "w2_high")}
-        for bank, v0 in (("first0", 0), ("chain", V // 2)):
-            acc = psum.tile([P, V // 2], F32, name="second", tag=bank, bufs=1)
-            multiply(acc[:], 1, w2_q, 0, v0, v0 + V // 2)
-            nc.scalar.activation(res[1, 0][:, v0 : v0 + V // 2], acc[:], RELU)
-        for t in range(1, PACK):
-            for sensor, wq in enumerate((w1_q, w2_q)):
-                res[sensor, t] = rectify(product(sensor, wq, t, "chain"), "res%d_%d" % (sensor, t), 0, V)
+        def product(sensor, t, bank="first1", tag=None):
+            acc = psum.tile([P, V], F32, name="acc", tag=bank, bufs=1)
+            multiply(acc[:], sensor, t, 0, V)
+            res[sensor, t] = sb([P, V], F32, "res%d_%d" % (sensor, t), tag)
+            nc.scalar.activation(res[sensor, t][:], acc[:], RELU)
+
+        product(1, 0)
+        settle("fourth", fourth, [(1, 1)])
+        scatter(1, 0, res[1, 0][:], 0, V)
+
+        late_planes = [(0, 2), (1, 2), (0, 3), (1, 3)]
+        late = sb([P, PACK * H], BF16, "late", "third_codes")
+        for place, (sensor, t) in enumerate(late_planes):
+            deal(nc.scalar.copy, late, place, raws[sensor], t)
+        settle("late", late, late_planes)
+        product(0, 1)
+        product(1, 1, "first0")
 
         starts = [sum(CHUNKS[:c]) for c in range(len(CHUNKS))]
         pairs = sb([P, PACK * S], BF16, "pairs")
@@ -177,19 +188,23 @@ def tile_picked_bev_max_p_kernel(
         def join_aside(t):
             halves = ((0, S // 2), (S // 2, S))
             excess = []
+            gap = sb([P, S], F32, "gap%d" % t, ("third_codes", "excess0_1", "late_scales")[t])
             for h, (r0, r1) in enumerate(halves):
-                gap = sb([P, S // 2], F32, "gap%d_%d" % (t, h))
-                excess.append(sb([P, S // 2], F32, "excess%d_%d" % (t, h)))
-                nc.gpsimd.tensor_tensor(gap[:], maps[0, t][:, r0:r1], maps[1, t][:, r0:r1], SUBTRACT)
-                nc.scalar.activation(excess[h][:], gap[:], RELU)
+                excess.append(sb([P, S // 2], F32, "excess%d_%d" % (t, h), ("late_codes", "late_scales")[h] if t == 1 else None))
+                nc.gpsimd.tensor_tensor(gap[:, r0:r1], maps[0, t][:, r0:r1], maps[1, t][:, r0:r1], SUBTRACT)
+                nc.scalar.activation(excess[h][:], gap[:, r0:r1], RELU)
             for h, (r0, r1) in enumerate(halves):
                 nc.gpsimd.tensor_tensor(slot(t, r0, r1), cells(excess[h], 0, S // 2), cells(maps[1, t], r0, r1), ADD)
 
-        scatter(1, 0, res[1, 0], 0, V)
         for t in range(1, PACK):
             join_aside(t - 1)
-            scatter(0, t, res[0, t], 0, V)
-            scatter(1, t, res[1, t], 0, V)
+            if t == 1:
+                product(0, 2, tag="third_codes")
+                product(1, 2, "first0")
+                product(0, 3)
+                product(1, 3, "first0")
+            scatter(0, t, res[0, t][:], 0, V)
+            scatter(1, t, res[1, t][:], 0, V)
 
         grouped = [sb([P, w, 2], U32, "z_grouped%d" % c) for c, w in enumerate(CHUNKS)]
 
@@ -198,17 +213,18 @@ def tile_picked_bev_max_p_kernel(
 
         def weave(c):
             r0, r1 = starts[c], starts[c] + CHUNKS[c]
-            words = pairs[:, PACK * r0 : PACK * r1].bitcast(U32).rearrange("p (b h r) -> p b r h", h=2, r=BLOCK)
-            nc.scalar.copy(grouped[c][:].rearrange("p (b r) h -> p b r h", r=BLOCK), words)
+            pair_words = pairs[:, PACK * r0 : PACK * r1].bitcast(U32).rearrange("p (b h r) -> p b r h", h=2, r=BLOCK)
+            nc.scalar.copy(grouped[c][:].rearrange("p (b r) h -> p b r h", r=BLOCK), pair_words)
 
         def finish(c):
             w = CHUNKS[c]
             zq = quantize(grouped[c][:].rearrange("p r h -> p (r h)").bitcast(BF16), w, "z%d" % c)
             acc = psum.tile([P, w], F32, name="acc_out")
+            codes, scales, col = quantised["w3"]
             nc.tensor.matmul_mx(
                 out=acc[:],
-                lhsT=w3_q[0][:].bitcast(FP8X4),
-                lhsT_scale=w3_q[1][:],
+                lhsT=codes[:, col : col + P].bitcast(FP8X4),
+                lhsT_scale=scales[:, col : col + P],
                 rhs=zq[0][:].bitcast(FP8X4),
                 rhs_scale=zq[1][:],
                 start=True,

@@ -21,6 +21,7 @@ P = 128
 PACK = 4
 BLOCK = 128
 SHARE = 8
+ASIDE = 64
 AHEAD = 512
 CHUNKS = (128, 256, 256, 256, 128)
 MAXIMA = (128, 256, 256, 384)
@@ -70,8 +71,10 @@ def tile_picked_bev_max_p_kernel(
 
         tiles = [sb([P, S], F32, "map%d" % b) for b in range(4)]
         nc.vector.memset(tiles[0][:], 0.0)
-        for b in (2, 1, 3):
+        nc.gpsimd.tensor_tensor(tiles[3][:, :ASIDE], tiles[0][:, :ASIDE], tiles[0][:, :ASIDE], SUBTRACT)
+        for b in (2, 1):
             nc.scalar.copy(tiles[b][:], tiles[0][:])
+        nc.scalar.copy(tiles[3][:, ASIDE:], tiles[0][:, ASIDE:])
         maps = {(sensor, n): tiles[2 * sensor + n % 2] for sensor in range(2) for n in range(PACK)}
 
         picked_scales = sb([P, S], U8, "picked_scales")

@@ -13,16 +13,13 @@ U16 = mybir.dt.uint16
 U8 = mybir.dt.uint8
 FP8X4 = mybir.dt.float8_e4m3fn_x4
 RELU = mybir.ActivationFunctionType.Relu
+COPY = mybir.ActivationFunctionType.Copy
 MAX = mybir.AluOpType.max
-ADD = mybir.AluOpType.add
-SUBTRACT = mybir.AluOpType.subtract
 
 P = 128
 PACK = 4
 BLOCK = 128
-SHARE = 8
-ASIDE = 64
-AHEAD = 512
+HALF = V // 2
 CHUNKS = (128, 256, 256, 256, 128)
 MAXIMA = (128, 256, 256, 384)
 
@@ -33,8 +30,7 @@ def tile_picked_bev_max_p_kernel(
     nc = tc.nc
     with ExitStack() as ctx:
         keep = ctx.enter_context(tc.tile_pool(name="keep", bufs=1))
-        reuse = ctx.enter_context(tc.tile_pool(name="reuse", bufs=1))
-        psum = ctx.enter_context(tc.psum_pool(name="psum", bufs=4))
+        psum = ctx.enter_context(tc.psum_pool(name="psum", bufs=1))
 
         def sb(shape, dtype, name, tag=None):
             return keep.tile(shape, dtype, name=name, tag=tag or name, align_bytes=64)
@@ -44,175 +40,158 @@ def tile_picked_bev_max_p_kernel(
         far_sb = sb([P, V // 16], U16, "far_sb")
         store_scales = sb([P, T], U8, "store_scales")
         store_words = sb([P, T], I32, "store_words")
+        raws = [sb([P, PACK, H], F32, "w%d_raw" % (s + 1)) for s in range(2)]
+        w3_raw = sb([P, PACK, N], F32, "w3_raw")
 
         nc.vector.memset(store_scales[:].bitcast(I32), 0)
         nc.sync.dma_start(offs_sb[:], offs)
-        words_in = x_words[0].rearrange("p c r -> p (c r)").bitcast(I32)
-        nc.sync.dma_start(store_words[:, :AHEAD], words_in[:, :AHEAD])
+        w1_rows = w1.rearrange("(p j) c -> p j c", j=PACK)
+        nc.sync.dma_start(raws[0][:, :1, :], w1_rows[:, :1, :])
         nc.sync.dma_start(near_sb[:], near)
         for q in range(4):
             nc.sync.dma_start(
                 store_scales[32 * q : 32 * q + 4, :].bitcast(I32), x_scales[0, 4 * q : 4 * q + 4, :].bitcast(I32)
             )
-
-        def load_weight(w, name):
-            raw = sb([P, PACK, H], F32, name + "_raw")
-            nc.sync.dma_start(raw[:], w.rearrange("(p j) c -> p j c", j=PACK))
-            return raw
-
-        nc.sync.dma_start(store_words[:, AHEAD:], words_in[:, AHEAD:])
-        w1_raw = load_weight(w1, "w1")
+        nc.sync.dma_start(raws[0][:, 1:, :], w1_rows[:, 1:, :])
+        nc.sync.dma_start(store_words[:], x_words[0].rearrange("p c r -> p (c r)").bitcast(I32))
+        nc.sync.dma_start(raws[1][:], w2.rearrange("(p j) c -> p j c", j=PACK))
         nc.sync.dma_start(far_sb[:], far)
-        w2_raw = load_weight(w2, "w2")
-        w3_raw = reuse.tile([P, PACK, N], F32, name="w3_raw", offset=0, align_bytes=64)
         w3_rows = w3.rearrange("(b t s) c -> t b s c", t=PACK, s=8)
         for t in range(PACK):
             nc.sync.dma_start(w3_raw[:, t, :], w3_rows[t])
 
-        tiles = [sb([P, S], F32, "map%d" % b) for b in range(4)]
-        nc.vector.memset(tiles[0][:], 0.0)
-        nc.gpsimd.tensor_tensor(tiles[3][:, :ASIDE], tiles[0][:, :ASIDE], tiles[0][:, :ASIDE], SUBTRACT)
-        for b in (2, 1):
+        tiles = [sb([P, S], F32, "map%d" % b) for b in range(6)]
+        for b in range(3):
+            nc.vector.memset(tiles[b][:], 0.0)
+        for b in range(3, 6):
             nc.scalar.copy(tiles[b][:], tiles[0][:])
-        nc.scalar.copy(tiles[3][:, ASIDE:], tiles[0][:, ASIDE:])
-        maps = {(sensor, n): tiles[2 * sensor + n % 2] for sensor in range(2) for n in range(PACK)}
+        maps = {(sensor, t): tiles[2 * (t % 3) + sensor] for sensor in range(2) for t in range(PACK)}
 
         picked_scales = sb([P, S], U8, "picked_scales")
         nc.vector.tensor_copy(picked_scales[:], store_scales[:].indirect(offs_sb[:]))
 
-        def deal(copy, grouped, place, raw, t, b0=0, b1=16):
-            plane = grouped[:, place * H : (place + 1) * H].rearrange("p (b s j) -> p b s j", s=8, j=PACK)
-            rows = raw[:].rearrange("p j (b t s) -> p t b s j", t=PACK, s=8)
-            copy(plane[:, b0:b1], rows[:, t, b0:b1])
+        grouped_w = [sb([P, PACK * H], BF16, "w%d_grouped" % (s + 1)) for s in range(2)]
+        codes_w = [sb([P, H], U32, "w%d_codes" % (s + 1)) for s in range(2)]
+        scales_w = [sb([P, H], U8, "w%d_scales" % (s + 1)) for s in range(2)]
 
-        def quantize(grouped_flat, width, name, tag=None):
-            codes = sb([P, width], U32, name + "_codes", tag)
-            scales = sb([P, width], U8, name + "_scales")
-            nc.vector.quantize_mx(out=codes[:].bitcast(FP8X4), scales=scales[:], in_=grouped_flat)
-            return codes, scales
+        def deal(copy, sensor, t):
+            plane = grouped_w[sensor][:, t * H : (t + 1) * H].rearrange("p (b s j) -> p b s j", s=8, j=PACK)
+            rows = raws[sensor][:].rearrange("p j (b t s) -> p t b s j", t=PACK, s=8)
+            copy(plane, rows[:, t])
 
-        def pick(name, c0, c1, tag=None):
-            pw = sb([P, c1 - c0], U32, name, tag)
-            nc.vector.tensor_copy(pw[:], store_words[:].bitcast(U32).indirect(offs_sb[:, c0 // 16 : c1 // 16]))
-            return pw
+        def settle(sensor, t0, t1):
+            nc.vector.quantize_mx(
+                out=codes_w[sensor][:, t0 * P : t1 * P].bitcast(FP8X4),
+                scales=scales_w[sensor][:, t0 * P : t1 * P],
+                in_=grouped_w[sensor][:, t0 * H : t1 * H],
+            )
 
-        raws = (w1_raw, w2_raw)
-        quantised = {}
+        for t in (0, 1):
+            deal(nc.scalar.copy, 0, t)
+        for t in (2, 3):
+            deal(nc.vector.tensor_copy, 0, t)
+        settle(0, 0, 2)
+        settle(0, 2, 4)
 
-        def prepare(name, planes):
-            grouped = sb([P, len(planes) * H], BF16, name)
-            for place, (sensor, t) in enumerate(planes):
-                deal(nc.scalar.copy, grouped, place, raws[sensor], t)
-            return grouped
+        picked_words = sb([P, S], U32, "picked_words")
 
-        def settle(name, grouped, planes):
-            made = quantize(grouped[:], len(planes) * P, name)
-            for place, key in enumerate(planes):
-                quantised[key] = made + (place * P,)
+        def pick(c0, c1):
+            nc.vector.tensor_copy(
+                picked_words[:, c0:c1], store_words[:].bitcast(U32).indirect(offs_sb[:, c0 // 16 : c1 // 16])
+            )
 
-        words0 = pick("words0", 0, V)
-        lead = sb([P, 2 * H], BF16, "lead")
-        deal(nc.vector.tensor_copy, lead, 0, w1_raw, 0, 0, SHARE)
-        deal(nc.scalar.copy, lead, 0, w1_raw, 0, SHARE, 16)
-        quantised[0, 0] = quantize(lead[:, :H], P, "lead") + (0,)
-        words = (words0, pick("words1", V, S, "lead"))
-
-        def multiply(acc, sensor, t, v0, v1):
-            codes, scales, col = quantised[sensor, t]
+        def multiply(bank, sensor, t, v0=0, v1=V):
+            acc = psum.tile([P, v1 - v0], F32, name="acc", tag="bank%d" % bank)
             nc.tensor.matmul_mx(
-                out=acc,
-                lhsT=codes[:, col : col + P].bitcast(FP8X4),
-                lhsT_scale=scales[:, col : col + P],
-                rhs=words[sensor][:, v0:v1].bitcast(FP8X4),
+                out=acc[:],
+                lhsT=codes_w[sensor][:, t * P : (t + 1) * P].bitcast(FP8X4),
+                lhsT_scale=scales_w[sensor][:, t * P : (t + 1) * P],
+                rhs=picked_words[:, sensor * V + v0 : sensor * V + v1].bitcast(FP8X4),
                 rhs_scale=picked_scales[:, sensor * V + v0 : sensor * V + v1],
                 start=True,
                 stop=True,
             )
+            return acc
 
+        pick(0, HALF)
+        pick(HALF, V)
+        first = [multiply(h, 0, 0, h * HALF, (h + 1) * HALF) for h in range(2)]
+        accs = {(0, t): multiply(1 + t, 0, t) for t in range(1, PACK)}
+        pick(V, S)
+
+        res = {(sensor, t): sb([P, V], F32, "res%d_%d" % (sensor, t)) for sensor in range(2) for t in range(PACK)}
         lists = (near_sb, far_sb)
 
-        def scatter(sensor, t, res, v0, v1):
-            nc.vector.tensor_copy(maps[sensor, t][:].indirect(lists[sensor][:, v0 // 16 : v1 // 16]), res)
+        def window(sensor, t, v0, v1):
+            return maps[sensor, t][:].indirect(lists[sensor][:, v0 // 16 : v1 // 16])
 
-        half = V // 2
-        first = [psum.tile([P, half], F32, name="first%d" % h, tag="first%d" % h, bufs=1) for h in range(2)]
+        def scatter_scalar(sensor, t, v0, v1):
+            nc.scalar.activation(window(sensor, t, v0, v1), res[sensor, t][:, v0:v1], COPY)
+
+        def scatter_vector(sensor, t, v0, v1):
+            nc.vector.tensor_copy(window(sensor, t, v0, v1), res[sensor, t][:, v0:v1])
+
+        def empty_scalar(sensor, t):
+            nc.scalar.activation(res[sensor, t][:], accs[sensor, t][:], RELU)
+
+        def empty_vector(sensor, t):
+            nc.vector.tensor_scalar_max(res[sensor, t][:], accs[sensor, t][:], 0.0)
+
         for h in range(2):
-            multiply(first[h][:], 0, 0, h * half, (h + 1) * half)
-        second = prepare("second", [(0, 1)])
-        head = sb([P, half], F32, "res_head")
-        nc.scalar.activation(head[:], first[0][:], RELU)
-        settle("second", second, [(0, 1)])
-        scatter(0, 0, head[:], 0, half)
+            nc.scalar.activation(res[0, 0][:, h * HALF : (h + 1) * HALF], first[h][:], RELU)
+        for h in range(2):
+            scatter_scalar(0, 0, h * HALF, (h + 1) * HALF)
 
-        third = prepare("third", [(1, 0)])
+        for t in range(PACK):
+            deal(nc.vector.tensor_copy, 1, t)
+        settle(1, 0, 1)
         w3_grouped = sb([P, N * PACK], BF16, "w3_grouped")
-        nc.scalar.copy(
+        nc.vector.tensor_copy(
             w3_grouped[:].rearrange("p (c a b) -> p c a b", a=2, b=2),
             w3_raw[:].rearrange("p (b a) c -> p c a b", a=2),
         )
-        rest = reuse.tile([P, half], F32, name="res_rest", offset=0, align_bytes=64)
-        nc.scalar.activation(rest[:], first[1][:], RELU)
-        settle("third", third, [(1, 0)])
-        settle("w3", w3_grouped, ["w3"])
-        scatter(0, 0, rest[:], half, V)
+        settle(1, 1, PACK)
+        w3_codes = sb([P, N], U32, "w3_codes")
+        w3_scales = sb([P, N], U8, "w3_scales")
+        nc.vector.quantize_mx(out=w3_codes[:].bitcast(FP8X4), scales=w3_scales[:], in_=w3_grouped[:])
+        for t in range(PACK):
+            accs[1, t] = multiply((5 + t) % 8, 1, t)
 
-        fourth = reuse.tile([P, H], BF16, name="fourth", offset=4 * half, align_bytes=64)
-        deal(nc.scalar.copy, fourth, 0, w2_raw, 1)
-        res = {}
-
-        def product(sensor, t, bank="first1", tag=None):
-            acc = psum.tile([P, V], F32, name="acc", tag=bank, bufs=1)
-            multiply(acc[:], sensor, t, 0, V)
-            res[sensor, t] = sb([P, V], F32, "res%d_%d" % (sensor, t), tag)
-            nc.scalar.activation(res[sensor, t][:], acc[:], RELU)
-
-        product(1, 0)
-        settle("fourth", fourth, [(1, 1)])
-        scatter(1, 0, res[1, 0][:], 0, V)
-
-        late_planes = [(0, 2), (1, 2), (0, 3), (1, 3)]
-        late = sb([P, PACK * H], BF16, "late", "third_codes")
-        for place, (sensor, t) in enumerate(late_planes):
-            deal(nc.scalar.copy, late, place, raws[sensor], t)
-        settle("late", late, late_planes)
-        product(0, 1)
-        product(1, 1, "first0")
-
-        starts = [sum(CHUNKS[:c]) for c in range(len(CHUNKS))]
         pairs = sb([P, PACK * S], BF16, "pairs")
         pair_view = pairs[:].rearrange("p (b h r e) -> p b h r e", h=2, r=BLOCK, e=2)
-
-        def slot(t, r0, r1):
-            return pair_view[:, r0 // BLOCK : r1 // BLOCK, t % 2, :, t // 2]
 
         def cells(tile, r0, r1):
             return tile[:, r0:r1].rearrange("p (b r) -> p b r", r=BLOCK)
 
-        def join_aside(t):
-            halves = ((0, S // 2), (S // 2, S))
-            excess = []
-            gap = sb([P, S], F32, "gap%d" % t, ("third_codes", "excess0_1", "late_scales")[t])
-            for h, (r0, r1) in enumerate(halves):
-                excess.append(sb([P, S // 2], F32, "excess%d_%d" % (t, h), ("late_codes", "late_scales")[h] if t == 1 else None))
-                nc.gpsimd.tensor_tensor(gap[:, r0:r1], maps[0, t][:, r0:r1], maps[1, t][:, r0:r1], SUBTRACT)
-                nc.scalar.activation(excess[h][:], gap[:, r0:r1], RELU)
-            for h, (r0, r1) in enumerate(halves):
-                nc.gpsimd.tensor_tensor(slot(t, r0, r1), cells(excess[h], 0, S // 2), cells(maps[1, t], r0, r1), ADD)
+        def join(t, r0=0, r1=S):
+            slot = pair_view[:, r0 // BLOCK : r1 // BLOCK, t % 2, :, t // 2]
+            nc.vector.tensor_tensor(slot, cells(maps[0, t], r0, r1), cells(maps[1, t], r0, r1), MAX)
 
-        for t in range(1, PACK):
-            join_aside(t - 1)
-            if t == 1:
-                product(0, 2, tag="third_codes")
-                product(1, 2, "first0")
-                product(0, 3)
-                product(1, 3, "first0")
-            scatter(0, t, res[0, t][:], 0, V)
-            scatter(1, t, res[1, t][:], 0, V)
+        def unit_scalar(sensor, t):
+            for h in range(2):
+                scatter_scalar(sensor, t, h * HALF, (h + 1) * HALF)
 
+        empty_vector(1, 0)
+        empty_vector(1, 1)
+        scatter_vector(1, 0, 0, V)
+        empty_scalar(0, 1)
+        empty_scalar(0, 2)
+        unit_scalar(0, 1)
+        scatter_vector(1, 1, 0, V)
+        empty_scalar(1, 2)
+        unit_scalar(0, 2)
+        join(0)
+        join(1)
+        empty_scalar(1, 3)
+        empty_scalar(0, 3)
+        unit_scalar(1, 2)
+        scatter_vector(1, 3, 0, HALF)
+        join(2)
+        scatter_vector(1, 3, HALF, V)
+        unit_scalar(0, 3)
+
+        starts = [sum(CHUNKS[:c]) for c in range(len(CHUNKS))]
         grouped = [sb([P, w, 2], U32, "z_grouped%d" % c) for c, w in enumerate(CHUNKS)]
-
-        def last_plane(r0, r1):
-            nc.vector.tensor_tensor(slot(3, r0, r1), cells(maps[0, 3], r0, r1), cells(maps[1, 3], r0, r1), MAX)
 
         def weave(c):
             r0, r1 = starts[c], starts[c] + CHUNKS[c]
@@ -221,15 +200,17 @@ def tile_picked_bev_max_p_kernel(
 
         def finish(c):
             w = CHUNKS[c]
-            zq = quantize(grouped[c][:].rearrange("p r h -> p (r h)").bitcast(BF16), w, "z%d" % c)
-            acc = psum.tile([P, w], F32, name="acc_out")
-            codes, scales, col = quantised["w3"]
+            codes = sb([P, w], U32, "z%d_codes" % c)
+            scales = sb([P, w], U8, "z%d_scales" % c)
+            flat = grouped[c][:].rearrange("p r h -> p (r h)").bitcast(BF16)
+            nc.vector.quantize_mx(out=codes[:].bitcast(FP8X4), scales=scales[:], in_=flat)
+            acc = psum.tile([P, w], F32, name="acc_out", tag="bank%d" % (1 + c))
             nc.tensor.matmul_mx(
                 out=acc[:],
-                lhsT=codes[:, col : col + P].bitcast(FP8X4),
-                lhsT_scale=scales[:, col : col + P],
-                rhs=zq[0][:].bitcast(FP8X4),
-                rhs_scale=zq[1][:],
+                lhsT=w3_codes[:].bitcast(FP8X4),
+                lhsT_scale=w3_scales[:],
+                rhs=codes[:].bitcast(FP8X4),
+                rhs_scale=scales[:],
                 start=True,
                 stop=True,
             )
@@ -243,9 +224,9 @@ def tile_picked_bev_max_p_kernel(
 
         n_chunks = len(CHUNKS)
         for m in range(len(MAXIMA)):
-            last_plane(sum(MAXIMA[:m]), sum(MAXIMA[: m + 1]))
+            join(3, sum(MAXIMA[:m]), sum(MAXIMA[: m + 1]))
         for c in range(n_chunks):
             weave(c)
-        accs = [finish(c) for c in range(n_chunks)]
+        outs = [finish(c) for c in range(n_chunks)]
         for c in range(n_chunks):
-            store(c, accs[c], nc.vector.tensor_copy if c >= n_chunks - 1 else nc.scalar.copy)
+            store(c, outs[c], nc.vector.tensor_copy if c >= n_chunks - 1 else nc.scalar.copy)

@@ -15,11 +15,19 @@ FP8X4 = mybir.dt.float8_e4m3fn_x4
 RELU = mybir.ActivationFunctionType.Relu
 COPY = mybir.ActivationFunctionType.Copy
 MAX = mybir.AluOpType.max
+MIN = mybir.AluOpType.min
+ADD = mybir.AluOpType.add
+MULT = mybir.AluOpType.mult
+SUBTRACT = mybir.AluOpType.subtract
+LARGEST = 3.4028234663852886e38
 
 P = 128
 PACK = 4
 BLOCK = 128
 HALF = V // 2
+AHEAD = 512
+PLANE = (0, 2, 1, 3)
+SLOT = (0, 2, 3, 1)
 CHUNKS = (128, 256, 256, 256, 128)
 MAXIMA = (128, 256, 256, 384)
 
@@ -45,150 +53,183 @@ def tile_picked_bev_max_p_kernel(
 
         nc.vector.memset(store_scales[:].bitcast(I32), 0)
         nc.sync.dma_start(offs_sb[:], offs)
-        w1_rows = w1.rearrange("(p j) c -> p j c", j=PACK)
-        nc.sync.dma_start(raws[0][:, :1, :], w1_rows[:, :1, :])
+        words_in = x_words[0].rearrange("p c r -> p (c r)").bitcast(I32)
+        nc.sync.dma_start(store_words[:, :AHEAD], words_in[:, :AHEAD])
         nc.sync.dma_start(near_sb[:], near)
         for q in range(4):
             nc.sync.dma_start(
                 store_scales[32 * q : 32 * q + 4, :].bitcast(I32), x_scales[0, 4 * q : 4 * q + 4, :].bitcast(I32)
             )
-        nc.sync.dma_start(raws[0][:, 1:, :], w1_rows[:, 1:, :])
-        nc.sync.dma_start(store_words[:], x_words[0].rearrange("p c r -> p (c r)").bitcast(I32))
-        nc.sync.dma_start(raws[1][:], w2.rearrange("(p j) c -> p j c", j=PACK))
+        nc.sync.dma_start(store_words[:, AHEAD:], words_in[:, AHEAD:])
+        for raw, w in zip(raws, (w1, w2)):
+            nc.sync.dma_start(raw[:], w.rearrange("(p j) c -> p j c", j=PACK))
         nc.sync.dma_start(far_sb[:], far)
         w3_rows = w3.rearrange("(b t s) c -> t b s c", t=PACK, s=8)
-        for t in range(PACK):
-            nc.sync.dma_start(w3_raw[:, t, :], w3_rows[t])
+        for n in range(PACK):
+            nc.sync.dma_start(w3_raw[:, SLOT[n], :], w3_rows[PLANE[n]])
 
-        tiles = [sb([P, S], F32, "map%d" % b) for b in range(6)]
-        for b in range(3):
+        tiles = [sb([P, S], F32, "map%d" % b) for b in range(7)]
+        for b in range(2):
             nc.vector.memset(tiles[b][:], 0.0)
-        for b in range(3, 6):
+        for b in range(2, 6):
             nc.scalar.copy(tiles[b][:], tiles[0][:])
-        maps = {(sensor, t): tiles[2 * (t % 3) + sensor] for sensor in range(2) for t in range(PACK)}
+        nc.gpsimd.tensor_scalar(tiles[6][:], tiles[1][:], 1.0, 0.0, MULT, ADD)
+        maps = {(sensor, n): tiles[2 * n + sensor] for sensor in range(2) for n in range(3)}
+        maps[0, 3], maps[1, 3] = tiles[0], tiles[6]
 
         picked_scales = sb([P, S], U8, "picked_scales")
         nc.vector.tensor_copy(picked_scales[:], store_scales[:].indirect(offs_sb[:]))
-
-        grouped_w = [sb([P, PACK * H], BF16, "w%d_grouped" % (s + 1)) for s in range(2)]
-        codes_w = [sb([P, H], U32, "w%d_codes" % (s + 1)) for s in range(2)]
-        scales_w = [sb([P, H], U8, "w%d_scales" % (s + 1)) for s in range(2)]
-
-        def deal(copy, sensor, t):
-            plane = grouped_w[sensor][:, t * H : (t + 1) * H].rearrange("p (b s j) -> p b s j", s=8, j=PACK)
-            rows = raws[sensor][:].rearrange("p j (b t s) -> p t b s j", t=PACK, s=8)
-            copy(plane, rows[:, t])
-
-        def settle(sensor, t0, t1):
-            nc.vector.quantize_mx(
-                out=codes_w[sensor][:, t0 * P : t1 * P].bitcast(FP8X4),
-                scales=scales_w[sensor][:, t0 * P : t1 * P],
-                in_=grouped_w[sensor][:, t0 * H : t1 * H],
-            )
-
-        for t in (0, 1):
-            deal(nc.scalar.copy, 0, t)
-        for t in (2, 3):
-            deal(nc.vector.tensor_copy, 0, t)
-        settle(0, 0, 2)
-        settle(0, 2, 4)
-
         picked_words = sb([P, S], U32, "picked_words")
+        nc.vector.tensor_copy(picked_words[:], store_words[:].bitcast(U32).indirect(offs_sb[:]))
 
-        def pick(c0, c1):
-            nc.vector.tensor_copy(
-                picked_words[:, c0:c1], store_words[:].bitcast(U32).indirect(offs_sb[:, c0 // 16 : c1 // 16])
+        stage = sb([P, 6 * H], BF16, "stage")
+
+        def round_gpsimd(dst, src):
+            nc.gpsimd.tensor_scalar(dst, src, 1.0, 0.0, MULT, ADD)
+
+        def deal(copy, place, sensor, n, count=1):
+            dst = stage[:, place * H : (place + count) * H].rearrange("p (t b r) -> p b t r", t=count, r=32)
+            rows = raws[sensor][:].rearrange("p j (b u) -> p b u j", u=32)
+            copy(dst, rows[:, :, 8 * PLANE[n] : 8 * (PLANE[n] + count), :])
+
+        quantised = {}
+
+        def settle(place, keys):
+            width = len(keys) * P
+            codes = sb([P, width], U32, "codes%d_%d" % (place, len(quantised)))
+            scales = sb([P, width], U8, "scales%d_%d" % (place, len(quantised)))
+            nc.vector.quantize_mx(
+                out=codes[:].bitcast(FP8X4), scales=scales[:], in_=stage[:, place * H : (place + len(keys)) * H]
             )
+            for i, key in enumerate(keys):
+                quantised[key] = (codes[:, i * P : (i + 1) * P].bitcast(FP8X4), scales[:, i * P : (i + 1) * P])
 
-        def multiply(bank, sensor, t, v0=0, v1=V):
-            acc = psum.tile([P, v1 - v0], F32, name="acc", tag="bank%d" % bank)
+        accs = {}
+
+        def multiply(bank, sensor, n, h0=0, h1=2):
+            acc = psum.tile([P, (h1 - h0) * HALF], F32, name="acc", tag="bank%d" % bank)
+            codes, scales = quantised[sensor, n]
+            picked = slice(sensor * V + h0 * HALF, sensor * V + h1 * HALF)
             nc.tensor.matmul_mx(
                 out=acc[:],
-                lhsT=codes_w[sensor][:, t * P : (t + 1) * P].bitcast(FP8X4),
-                lhsT_scale=scales_w[sensor][:, t * P : (t + 1) * P],
-                rhs=picked_words[:, sensor * V + v0 : sensor * V + v1].bitcast(FP8X4),
-                rhs_scale=picked_scales[:, sensor * V + v0 : sensor * V + v1],
+                lhsT=codes,
+                lhsT_scale=scales,
+                rhs=picked_words[:, picked].bitcast(FP8X4),
+                rhs_scale=picked_scales[:, picked],
                 start=True,
                 stop=True,
             )
-            return acc
+            accs[sensor, n, h0, h1] = acc[:]
+            for h in range(h0, h1):
+                accs[sensor, n, h, h + 1] = acc[:, (h - h0) * HALF : (h - h0 + 1) * HALF]
 
-        pick(0, HALF)
-        pick(HALF, V)
-        first = [multiply(h, 0, 0, h * HALF, (h + 1) * HALF) for h in range(2)]
-        accs = {(0, t): multiply(1 + t, 0, t) for t in range(1, PACK)}
-        pick(V, S)
-
-        res = {(sensor, t): sb([P, V], F32, "res%d_%d" % (sensor, t)) for sensor in range(2) for t in range(PACK)}
         lists = (near_sb, far_sb)
+        res = {}
 
-        def window(sensor, t, v0, v1):
-            return maps[sensor, t][:].indirect(lists[sensor][:, v0 // 16 : v1 // 16])
+        def empty(engine, sensor, n, h0=0, h1=2, tile=None):
+            if tile is None:
+                tile = sb([P, (h1 - h0) * HALF], F32, "res%d_%d_%d" % (sensor, n, h0))[:]
+            src = accs[sensor, n, h0, h1]
+            if engine == "scalar":
+                nc.scalar.activation(tile, src, RELU)
+            else:
+                nc.vector.tensor_scalar_max(tile, src, 0.0)
+            for h in range(h0, h1):
+                res[sensor, n, h] = tile[:, (h - h0) * HALF : (h - h0 + 1) * HALF]
+            res[sensor, n] = tile
 
-        def scatter_scalar(sensor, t, v0, v1):
-            nc.scalar.activation(window(sensor, t, v0, v1), res[sensor, t][:, v0:v1], COPY)
+        def window(sensor, n, h0, h1):
+            return maps[sensor, n][:].indirect(lists[sensor][:, h0 * HALF // 16 : h1 * HALF // 16])
 
-        def scatter_vector(sensor, t, v0, v1):
-            nc.vector.tensor_copy(window(sensor, t, v0, v1), res[sensor, t][:, v0:v1])
+        def scatter_scalar(sensor, n, halves=(0, 1)):
+            for h in halves:
+                nc.scalar.activation(window(sensor, n, h, h + 1), res[sensor, n, h], COPY)
 
-        def empty_scalar(sensor, t):
-            nc.scalar.activation(res[sensor, t][:], accs[sensor, t][:], RELU)
+        def scatter_vector(sensor, n, h=None):
+            if h is None:
+                nc.vector.tensor_copy(window(sensor, n, 0, 2), res[sensor, n])
+            else:
+                nc.vector.tensor_copy(window(sensor, n, h, h + 1), res[sensor, n, h])
 
-        def empty_vector(sensor, t):
-            nc.vector.tensor_scalar_max(res[sensor, t][:], accs[sensor, t][:], 0.0)
-
+        deal(nc.scalar.copy, 4, 0, 0)
+        deal(round_gpsimd, 3, 0, 1)
+        deal(nc.scalar.copy, 5, 0, 2)
+        settle(3, [(0, 1), (0, 0)])
         for h in range(2):
-            nc.scalar.activation(res[0, 0][:, h * HALF : (h + 1) * HALF], first[h][:], RELU)
+            for n in range(2):
+                multiply(2 * h + n, 0, n, h, h + 1)
+        settle(5, [(0, 2)])
+        multiply(4, 0, 2)
+        empty("scalar", 0, 0, 0, 1)
+        empty("scalar", 0, 1, 0, 1)
+        empty("vector", 0, 0, 1, 2)
+        deal(round_gpsimd, 3, 0, 3)
+        deal(round_gpsimd, 0, 1, 0, 2)
+        scatter_scalar(0, 0, (0,))
+        scatter_vector(0, 1, 0)
+        empty("scalar", 0, 1, 1, 2)
+        scatter_scalar(0, 0, (1,))
+        settle(0, [(1, 0)])
+        settle(1, [(1, 2)])
         for h in range(2):
-            scatter_scalar(0, 0, h * HALF, (h + 1) * HALF)
-
-        for t in range(PACK):
-            deal(nc.vector.tensor_copy, 1, t)
-        settle(1, 0, 1)
-        w3_grouped = sb([P, N * PACK], BF16, "w3_grouped")
-        nc.vector.tensor_copy(
-            w3_grouped[:].rearrange("p (c a b) -> p c a b", a=2, b=2),
-            w3_raw[:].rearrange("p (b a) c -> p c a b", a=2),
-        )
-        settle(1, 1, PACK)
-        w3_codes = sb([P, N], U32, "w3_codes")
-        w3_scales = sb([P, N], U8, "w3_scales")
-        nc.vector.quantize_mx(out=w3_codes[:].bitcast(FP8X4), scales=w3_scales[:], in_=w3_grouped[:])
-        for t in range(PACK):
-            accs[1, t] = multiply((5 + t) % 8, 1, t)
+            multiply(5 + h, 1, 0, h, h + 1)
+        multiply(7, 1, 2)
+        round_gpsimd(stage[:, :H].rearrange("p (c a) -> p c a", a=PACK), w3_raw[:].rearrange("p a c -> p c a"))
+        deal(round_gpsimd, 1, 1, 1, 2)
+        shared = sb([P, V], F32, "shared")
+        empty("vector", 1, 0, 0, 1, shared[:, :HALF])
+        empty("vector", 1, 0, 1, 2)
+        scatter_scalar(0, 1, (1,))
+        scatter_vector(1, 0, 0)
+        settle(0, ["w3", (1, 1)])
+        settle(2, [(1, 3), (0, 3)])
+        w3_codes, w3_scales = quantised["w3"]
+        for bank, key in enumerate(((1, 1), (1, 3), (0, 3))):
+            multiply(bank, *key)
+        scatter_scalar(1, 0, (1,))
 
         pairs = sb([P, PACK * S], BF16, "pairs")
         pair_view = pairs[:].rearrange("p (b h r e) -> p b h r e", h=2, r=BLOCK, e=2)
+        excess_view = pairs[:].bitcast(F32).rearrange("p (b h r) -> p b h r", h=2, r=BLOCK)
 
         def cells(tile, r0, r1):
             return tile[:, r0:r1].rearrange("p (b r) -> p b r", r=BLOCK)
 
-        def join(t, r0=0, r1=S):
-            slot = pair_view[:, r0 // BLOCK : r1 // BLOCK, t % 2, :, t // 2]
-            nc.vector.tensor_tensor(slot, cells(maps[0, t], r0, r1), cells(maps[1, t], r0, r1), MAX)
+        def slot(n, r0, r1):
+            return pair_view[:, r0 // BLOCK : r1 // BLOCK, SLOT[n] // 2, :, SLOT[n] % 2]
 
-        def unit_scalar(sensor, t):
-            for h in range(2):
-                scatter_scalar(sensor, t, h * HALF, (h + 1) * HALF)
+        def join(n, r0=0, r1=S):
+            nc.vector.tensor_tensor(slot(n, r0, r1), cells(maps[0, n], r0, r1), cells(maps[1, n], r0, r1), MAX)
 
-        empty_vector(1, 0)
-        empty_vector(1, 1)
-        scatter_vector(1, 0, 0, V)
-        empty_scalar(0, 1)
-        empty_scalar(0, 2)
-        unit_scalar(0, 1)
-        scatter_vector(1, 1, 0, V)
-        empty_scalar(1, 2)
-        unit_scalar(0, 2)
-        join(0)
+        halves = ((0, S // 2), (S // 2, S))
+        gap = sb([P, S], F32, "gap")
+        for r0, r1 in halves:
+            nc.gpsimd.tensor_tensor(gap[:, r0:r1], maps[1, 0][:, r0:r1], maps[0, 0][:, r0:r1], SUBTRACT)
+        for r0, r1 in halves:
+            excess = excess_view[:, r0 // BLOCK : r1 // BLOCK, 1, :]
+            nc.gpsimd.tensor_scalar(excess, cells(gap, r0, r1), LARGEST, 0.0, MIN, MAX)
+        for r0, r1 in halves:
+            excess = excess_view[:, r0 // BLOCK : r1 // BLOCK, 1, :]
+            nc.gpsimd.tensor_tensor(slot(0, r0, r1), excess, cells(maps[0, 0], r0, r1), ADD)
+
+        empty("vector", 1, 1)
+        after_shared = sb([P, V], F32, "after_shared", "shared")
+        for h in range(2):
+            empty("scalar", 0, 2, h, h + 1, after_shared[:, h * HALF : (h + 1) * HALF])
+        late = sb([P, 2 * V], F32, "late", "stage")
+        empty("vector", 1, 3)
+        empty("vector", 1, 2, 0, 2, late[:, :V])
+        scatter_vector(1, 1)
+        for h in range(2):
+            scatter_scalar(0, 2, (h,))
+            scatter_scalar(1, 3, (h,))
+        empty("vector", 0, 3, 0, 1, late[:, V : V + HALF])
+        scatter_vector(1, 2)
+        scatter_scalar(0, 3, (0,))
+        empty("scalar", 0, 3, 1, 2)
+        scatter_scalar(0, 3, (1,))
         join(1)
-        empty_scalar(1, 3)
-        empty_scalar(0, 3)
-        unit_scalar(1, 2)
-        scatter_vector(1, 3, 0, HALF)
         join(2)
-        scatter_vector(1, 3, HALF, V)
-        unit_scalar(0, 3)
 
         starts = [sum(CHUNKS[:c]) for c in range(len(CHUNKS))]
         grouped = [sb([P, w, 2], U32, "z_grouped%d" % c) for c, w in enumerate(CHUNKS)]
@@ -204,11 +245,11 @@ def tile_picked_bev_max_p_kernel(
             scales = sb([P, w], U8, "z%d_scales" % c)
             flat = grouped[c][:].rearrange("p r h -> p (r h)").bitcast(BF16)
             nc.vector.quantize_mx(out=codes[:].bitcast(FP8X4), scales=scales[:], in_=flat)
-            acc = psum.tile([P, w], F32, name="acc_out", tag="bank%d" % (1 + c))
+            acc = psum.tile([P, w], F32, name="acc_out", tag="bank%d" % (3 + c))
             nc.tensor.matmul_mx(
                 out=acc[:],
-                lhsT=w3_codes[:].bitcast(FP8X4),
-                lhsT_scale=w3_scales[:],
+                lhsT=w3_codes,
+                lhsT_scale=w3_scales,
                 rhs=codes[:].bitcast(FP8X4),
                 rhs_scale=scales[:],
                 start=True,

@@ -38,10 +38,14 @@ def tile_picked_bev_max_p_kernel(
     nc = tc.nc
     with ExitStack() as ctx:
         keep = ctx.enter_context(tc.tile_pool(name="keep", bufs=1))
+        reuse = ctx.enter_context(tc.tile_pool(name="reuse", bufs=1))
         psum = ctx.enter_context(tc.psum_pool(name="psum", bufs=1))
 
         def sb(shape, dtype, name, tag=None):
             return keep.tile(shape, dtype, name=name, tag=tag or name, align_bytes=64)
+
+        def placed(shape, dtype, name, offset):
+            return reuse.tile(shape, dtype, name=name, offset=offset, align_bytes=64)
 
         offs_sb = sb([P, S // 16], U16, "offs_sb")
         near_sb = sb([P, V // 16], U16, "near_sb")
@@ -68,38 +72,44 @@ def tile_picked_bev_max_p_kernel(
         for n in range(PACK):
             nc.sync.dma_start(w3_raw[:, SLOT[n], :], w3_rows[PLANE[n]])
 
-        tiles = [sb([P, S], F32, "map%d" % b) for b in range(7)]
+        tiles = [sb([P, S], F32, "map%d" % b) for b in range(8)]
         for b in range(2):
             nc.vector.memset(tiles[b][:], 0.0)
         for b in range(2, 6):
             nc.scalar.copy(tiles[b][:], tiles[0][:])
-        nc.gpsimd.tensor_scalar(tiles[6][:], tiles[1][:], 1.0, 0.0, MULT, ADD)
-        maps = {(sensor, n): tiles[2 * n + sensor] for sensor in range(2) for n in range(3)}
-        maps[0, 3], maps[1, 3] = tiles[0], tiles[6]
+        for b in range(6, 8):
+            nc.gpsimd.tensor_scalar(tiles[b][:], tiles[1][:], 1.0, 0.0, MULT, ADD)
+        maps = {(sensor, n): tiles[2 * n + sensor] for sensor in range(2) for n in range(PACK)}
 
         picked_scales = sb([P, S], U8, "picked_scales")
         nc.vector.tensor_copy(picked_scales[:], store_scales[:].indirect(offs_sb[:]))
-        picked_words = sb([P, S], U32, "picked_words")
-        nc.vector.tensor_copy(picked_words[:], store_words[:].bitcast(U32).indirect(offs_sb[:]))
 
-        stage = sb([P, 6 * H], BF16, "stage")
+        def pick(picked, c0, c1):
+            nc.vector.tensor_copy(picked[:], store_words[:].bitcast(U32).indirect(offs_sb[:, c0 // 16 : c1 // 16]))
+            return picked
+
+        early = pick(sb([P, S - HALF], U32, "early_words"), 0, S - HALF)
+        words = {divmod(g, 2): early[:, g * HALF : (g + 1) * HALF] for g in range(3)}
+
+        lead = placed([P, 2 * H], BF16, "lead", 0)
+        stage = placed([P, 4 * H], BF16, "stage", 2 * H)
 
         def round_gpsimd(dst, src):
             nc.gpsimd.tensor_scalar(dst, src, 1.0, 0.0, MULT, ADD)
 
-        def deal(copy, place, sensor, n, count=1):
-            dst = stage[:, place * H : (place + count) * H].rearrange("p (t b r) -> p b t r", t=count, r=32)
+        def deal(copy, place, sensor, n, count=1, tile=stage):
+            dst = tile[:, place * H : (place + count) * H].rearrange("p (t b r) -> p b t r", t=count, r=32)
             rows = raws[sensor][:].rearrange("p j (b u) -> p b u j", u=32)
             copy(dst, rows[:, :, 8 * PLANE[n] : 8 * (PLANE[n] + count), :])
 
         quantised = {}
 
-        def settle(place, keys):
+        def settle(place, keys, tile=stage):
             width = len(keys) * P
             codes = sb([P, width], U32, "codes%d_%d" % (place, len(quantised)))
             scales = sb([P, width], U8, "scales%d_%d" % (place, len(quantised)))
             nc.vector.quantize_mx(
-                out=codes[:].bitcast(FP8X4), scales=scales[:], in_=stage[:, place * H : (place + len(keys)) * H]
+                out=codes[:].bitcast(FP8X4), scales=scales[:], in_=tile[:, place * H : (place + len(keys)) * H]
             )
             for i, key in enumerate(keys):
                 quantised[key] = (codes[:, i * P : (i + 1) * P].bitcast(FP8X4), scales[:, i * P : (i + 1) * P])
@@ -109,16 +119,18 @@ def tile_picked_bev_max_p_kernel(
         def multiply(bank, sensor, n, h0=0, h1=2):
             acc = psum.tile([P, (h1 - h0) * HALF], F32, name="acc", tag="bank%d" % bank)
             codes, scales = quantised[sensor, n]
-            picked = slice(sensor * V + h0 * HALF, sensor * V + h1 * HALF)
-            nc.tensor.matmul_mx(
-                out=acc[:],
-                lhsT=codes,
-                lhsT_scale=scales,
-                rhs=picked_words[:, picked].bitcast(FP8X4),
-                rhs_scale=picked_scales[:, picked],
-                start=True,
-                stop=True,
-            )
+            runs = [(h0, h1)] if sensor == 0 else [(h, h + 1) for h in range(h0, h1)]
+            for a, b in runs:
+                moving = early[:, a * HALF : b * HALF] if sensor == 0 else words[1, a]
+                nc.tensor.matmul_mx(
+                    out=acc[:, (a - h0) * HALF : (b - h0) * HALF],
+                    lhsT=codes,
+                    lhsT_scale=scales,
+                    rhs=moving.bitcast(FP8X4),
+                    rhs_scale=picked_scales[:, sensor * V + a * HALF : sensor * V + b * HALF],
+                    start=True,
+                    stop=True,
+                )
             accs[sensor, n, h0, h1] = acc[:]
             for h in range(h0, h1):
                 accs[sensor, n, h, h + 1] = acc[:, (h - h0) * HALF : (h - h0 + 1) * HALF]
@@ -151,33 +163,32 @@ def tile_picked_bev_max_p_kernel(
             else:
                 nc.vector.tensor_copy(window(sensor, n, h, h + 1), res[sensor, n, h])
 
-        deal(nc.scalar.copy, 4, 0, 0)
-        deal(round_gpsimd, 3, 0, 1)
-        deal(nc.scalar.copy, 5, 0, 2)
-        settle(3, [(0, 1), (0, 0)])
+        deal(nc.scalar.copy, 0, 0, 0, 1, lead)
+        deal(round_gpsimd, 1, 0, 1, 1, lead)
+        settle(0, [(0, 0), (0, 1)], lead)
         for h in range(2):
             for n in range(2):
                 multiply(2 * h + n, 0, n, h, h + 1)
-        settle(5, [(0, 2)])
-        multiply(4, 0, 2)
+        deal(nc.scalar.copy, 3, 0, 3)
+        words[1, 1] = pick(placed([P, HALF], U32, "last_words", 0), S - HALF, S)[:]
         empty("scalar", 0, 0, 0, 1)
         empty("scalar", 0, 1, 0, 1)
         empty("vector", 0, 0, 1, 2)
-        deal(round_gpsimd, 3, 0, 3)
+        deal(round_gpsimd, 2, 0, 2)
         deal(round_gpsimd, 0, 1, 0, 2)
         scatter_scalar(0, 0, (0,))
         scatter_vector(0, 1, 0)
         empty("scalar", 0, 1, 1, 2)
         scatter_scalar(0, 0, (1,))
         settle(0, [(1, 0)])
-        settle(1, [(1, 2)])
+        settle(1, [(1, 2), (0, 2)])
         for h in range(2):
             multiply(5 + h, 1, 0, h, h + 1)
+        multiply(4, 0, 2)
         multiply(7, 1, 2)
         round_gpsimd(stage[:, :H].rearrange("p (c a) -> p c a", a=PACK), w3_raw[:].rearrange("p a c -> p c a"))
         deal(round_gpsimd, 1, 1, 1, 2)
-        shared = sb([P, V], F32, "shared")
-        empty("vector", 1, 0, 0, 1, shared[:, :HALF])
+        empty("vector", 1, 0, 0, 1)
         empty("vector", 1, 0, 1, 2)
         scatter_scalar(0, 1, (1,))
         scatter_vector(1, 0, 0)
@@ -212,13 +223,11 @@ def tile_picked_bev_max_p_kernel(
             excess = excess_view[:, r0 // BLOCK : r1 // BLOCK, 1, :]
             nc.gpsimd.tensor_tensor(slot(0, r0, r1), excess, cells(maps[0, 0], r0, r1), ADD)
 
-        empty("vector", 1, 1)
-        after_shared = sb([P, V], F32, "after_shared", "shared")
-        for h in range(2):
-            empty("scalar", 0, 2, h, h + 1, after_shared[:, h * HALF : (h + 1) * HALF])
-        late = sb([P, 2 * V], F32, "late", "stage")
-        empty("vector", 1, 3)
+        late = placed([P, 3 * V], F32, "late", 2 * H)
+        empty("vector", 0, 2, 0, 2, late[:, 2 * V :])
         empty("vector", 1, 2, 0, 2, late[:, :V])
+        empty("vector", 1, 1)
+        empty("vector", 1, 3)
         scatter_vector(1, 1)
         for h in range(2):
             scatter_scalar(0, 2, (h,))
@@ -226,7 +235,7 @@ def tile_picked_bev_max_p_kernel(
         empty("vector", 0, 3, 0, 1, late[:, V : V + HALF])
         scatter_vector(1, 2)
         scatter_scalar(0, 3, (0,))
-        empty("scalar", 0, 3, 1, 2)
+        empty("scalar", 0, 3, 1, 2, sb([P, S], F32, "last_piece", "map0")[:, :HALF])
         scatter_scalar(0, 3, (1,))
         join(1)
         join(2)

@@ -164,7 +164,7 @@ def tile_picked_bev_max_p_kernel(
                 nc.vector.tensor_copy(window(sensor, n, h, h + 1), res[sensor, n, h])
 
         deal(nc.scalar.copy, 0, 0, 0, 1, lead)
-        deal(round_gpsimd, 1, 0, 1, 1, lead)
+        deal(nc.vector.tensor_copy, 1, 0, 1, 1, lead)
         settle(0, [(0, 0), (0, 1)], lead)
         for h in range(2):
             for n in range(2):
@@ -186,7 +186,7 @@ def tile_picked_bev_max_p_kernel(
             multiply(5 + h, 1, 0, h, h + 1)
         multiply(4, 0, 2)
         multiply(7, 1, 2)
-        round_gpsimd(stage[:, :H].rearrange("p (c a) -> p c a", a=PACK), w3_raw[:].rearrange("p a c -> p c a"))
+        nc.vector.tensor_copy(stage[:, :H].rearrange("p (c a) -> p c a", a=PACK), w3_raw[:].rearrange("p a c -> p c a"))
         deal(round_gpsimd, 1, 1, 1, 2)
         empty("vector", 1, 0, 0, 1)
         empty("vector", 1, 0, 1, 2)

@@ -26,6 +26,7 @@ PACK = 4
 BLOCK = 128
 HALF = V // 2
 AHEAD = 512
+CUT = 128
 PLANE = (0, 2, 1, 3)
 SLOT = (0, 2, 3, 1)
 CHUNKS = (128, 256, 256, 256, 128)
@@ -38,14 +39,10 @@ def tile_picked_bev_max_p_kernel(
     nc = tc.nc
     with ExitStack() as ctx:
         keep = ctx.enter_context(tc.tile_pool(name="keep", bufs=1))
-        reuse = ctx.enter_context(tc.tile_pool(name="reuse", bufs=1))
         psum = ctx.enter_context(tc.psum_pool(name="psum", bufs=1))
 
         def sb(shape, dtype, name, tag=None):
             return keep.tile(shape, dtype, name=name, tag=tag or name, align_bytes=64)
-
-        def placed(shape, dtype, name, offset):
-            return reuse.tile(shape, dtype, name=name, offset=offset, align_bytes=64)
 
         offs_sb = sb([P, S // 16], U16, "offs_sb")
         near_sb = sb([P, V // 16], U16, "near_sb")
@@ -91,8 +88,8 @@ def tile_picked_bev_max_p_kernel(
         early = pick(sb([P, S - HALF], U32, "early_words"), 0, S - HALF)
         words = {divmod(g, 2): early[:, g * HALF : (g + 1) * HALF] for g in range(3)}
 
-        lead = placed([P, 2 * H], BF16, "lead", 0)
-        stage = placed([P, 4 * H], BF16, "stage", 2 * H)
+        lead = sb([P, 2 * H], BF16, "lead")
+        stage = sb([P, 4 * H], BF16, "stage")
 
         def round_gpsimd(dst, src):
             nc.gpsimd.tensor_scalar(dst, src, 1.0, 0.0, MULT, ADD)
@@ -169,12 +166,12 @@ def tile_picked_bev_max_p_kernel(
         for h in range(2):
             for n in range(2):
                 multiply(2 * h + n, 0, n, h, h + 1)
-        deal(nc.scalar.copy, 3, 0, 3)
-        words[1, 1] = pick(placed([P, HALF], U32, "last_words", 0), S - HALF, S)[:]
+        for n in (2, 3):
+            deal(nc.scalar.copy, n, 0, n)
+        words[1, 1] = pick(sb([P, HALF], U32, "last_words", "lead"), S - HALF, S)[:]
         empty("scalar", 0, 0, 0, 1)
         empty("scalar", 0, 1, 0, 1)
         empty("vector", 0, 0, 1, 2)
-        deal(round_gpsimd, 2, 0, 2)
         deal(round_gpsimd, 0, 1, 0, 2)
         scatter_scalar(0, 0, (0,))
         scatter_vector(0, 1, 0)
@@ -223,20 +220,25 @@ def tile_picked_bev_max_p_kernel(
             excess = excess_view[:, r0 // BLOCK : r1 // BLOCK, 1, :]
             nc.gpsimd.tensor_tensor(slot(0, r0, r1), excess, cells(maps[0, 0], r0, r1), ADD)
 
-        late = placed([P, 3 * V], F32, "late", 2 * H)
-        empty("vector", 0, 2, 0, 2, late[:, 2 * V :])
+        late = sb([P, 2 * V], F32, "late", "stage")
         empty("vector", 1, 2, 0, 2, late[:, :V])
         empty("vector", 1, 1)
-        empty("vector", 1, 3)
         scatter_vector(1, 1)
         for h in range(2):
-            scatter_scalar(0, 2, (h,))
-            scatter_scalar(1, 3, (h,))
-        empty("vector", 0, 3, 0, 1, late[:, V : V + HALF])
+            empty("scalar", 0, 2, h, h + 1, late[:, V + h * HALF : V + (h + 1) * HALF])
+        scatter_scalar(0, 2, (0,))
+        for h in range(2):
+            empty("scalar", 1, 3, h, h + 1)
+        scatter_scalar(1, 3, (0,))
+        scatter_scalar(0, 2, (1,))
+        cut_piece = sb([P, CUT], F32, "cut_piece")
+        nc.scalar.activation(cut_piece[:], accs[0, 3, 0, 2][:, :CUT], RELU)
+        scatter_scalar(1, 3, (1,))
         scatter_vector(1, 2)
-        scatter_scalar(0, 3, (0,))
-        empty("scalar", 0, 3, 1, 2, sb([P, S], F32, "last_piece", "map0")[:, :HALF])
-        scatter_scalar(0, 3, (1,))
+        nc.vector.tensor_copy(maps[0, 3][:].indirect(near_sb[:, : CUT // 16]), cut_piece[:])
+        last_piece = sb([P, S], F32, "last_piece", "map0")[:, : V - CUT]
+        nc.scalar.activation(last_piece, accs[0, 3, 0, 2][:, CUT:], RELU)
+        nc.scalar.activation(maps[0, 3][:].indirect(near_sb[:, CUT // 16 :]), last_piece, COPY)
         join(1)
         join(2)
 

@@ -39,10 +39,14 @@ def tile_picked_bev_max_p_kernel(
     nc = tc.nc
     with ExitStack() as ctx:
         keep = ctx.enter_context(tc.tile_pool(name="keep", bufs=1))
+        reuse = ctx.enter_context(tc.tile_pool(name="reuse", bufs=1))
         psum = ctx.enter_context(tc.psum_pool(name="psum", bufs=1))
 
         def sb(shape, dtype, name, tag=None):
             return keep.tile(shape, dtype, name=name, tag=tag or name, align_bytes=64)
+
+        def placed(shape, dtype, name, offset):
+            return reuse.tile(shape, dtype, name=name, offset=offset, align_bytes=64)
 
         offs_sb = sb([P, S // 16], U16, "offs_sb")
         near_sb = sb([P, V // 16], U16, "near_sb")
@@ -88,7 +92,7 @@ def tile_picked_bev_max_p_kernel(
         early = pick(sb([P, S - HALF], U32, "early_words"), 0, S - HALF)
         words = {divmod(g, 2): early[:, g * HALF : (g + 1) * HALF] for g in range(3)}
 
-        lead = sb([P, 2 * H], BF16, "lead")
+        lead = placed([P, 2 * H], BF16, "lead", 0)
         stage = sb([P, 4 * H], BF16, "stage")
 
         def round_gpsimd(dst, src):
@@ -101,9 +105,9 @@ def tile_picked_bev_max_p_kernel(
 
         quantised = {}
 
-        def settle(place, keys, tile=stage):
+        def settle(place, keys, tile=stage, tag=None):
             width = len(keys) * P
-            codes = sb([P, width], U32, "codes%d_%d" % (place, len(quantised)))
+            codes = sb([P, width], U32, "codes%d_%d" % (place, len(quantised)), tag)
             scales = sb([P, width], U8, "scales%d_%d" % (place, len(quantised)))
             nc.vector.quantize_mx(
                 out=codes[:].bitcast(FP8X4), scales=scales[:], in_=tile[:, place * H : (place + len(keys)) * H]
@@ -166,26 +170,28 @@ def tile_picked_bev_max_p_kernel(
         for h in range(2):
             for n in range(2):
                 multiply(2 * h + n, 0, n, h, h + 1)
-        for n in (2, 3):
-            deal(nc.scalar.copy, n, 0, n)
-        words[1, 1] = pick(sb([P, HALF], U32, "last_words", "lead"), S - HALF, S)[:]
+        deal(nc.scalar.copy, 3, 0, 3)
+        words[1, 1] = pick(placed([P, HALF], U32, "last_words", 0), S - HALF, S)[:]
         empty("scalar", 0, 0, 0, 1)
         empty("scalar", 0, 1, 0, 1)
         empty("vector", 0, 0, 1, 2)
+        third = placed([P, H], BF16, "third", 2 * H)
+        deal(round_gpsimd, 0, 0, 2, 1, third)
         deal(round_gpsimd, 0, 1, 0, 2)
         scatter_scalar(0, 0, (0,))
         scatter_vector(0, 1, 0)
         empty("scalar", 0, 1, 1, 2)
         scatter_scalar(0, 0, (1,))
         settle(0, [(1, 0)])
-        settle(1, [(1, 2), (0, 2)])
+        settle(1, [(1, 2)])
+        settle(0, [(0, 2)], third, "res0_0_0")
         for h in range(2):
             multiply(5 + h, 1, 0, h, h + 1)
-        multiply(4, 0, 2)
         multiply(7, 1, 2)
         nc.vector.tensor_copy(stage[:, :H].rearrange("p (c a) -> p c a", a=PACK), w3_raw[:].rearrange("p a c -> p c a"))
         deal(round_gpsimd, 1, 1, 1, 2)
         empty("vector", 1, 0, 0, 1)
+        multiply(5, 0, 2)
         empty("vector", 1, 0, 1, 2)
         scatter_scalar(0, 1, (1,))
         scatter_vector(1, 0, 0)

@@ -26,7 +26,7 @@ PACK = 4
 BLOCK = 128
 HALF = V // 2
 AHEAD = 512
-CUT = 128
+CUT = 160
 PLANE = (0, 2, 1, 3)
 SLOT = (0, 2, 3, 1)
 CHUNKS = (128, 256, 256, 256, 128)
@@ -73,7 +73,7 @@ def tile_picked_bev_max_p_kernel(
         for n in range(PACK):
             nc.sync.dma_start(w3_raw[:, SLOT[n], :], w3_rows[PLANE[n]])
 
-        tiles = [sb([P, S], F32, "map%d" % b) for b in range(8)]
+        tiles = [placed([P, S], F32, "map0", 4 * H)] + [sb([P, S], F32, "map%d" % b) for b in range(1, 8)]
         for b in range(2):
             nc.vector.memset(tiles[b][:], 0.0)
         for b in range(2, 6):
@@ -188,16 +188,16 @@ def tile_picked_bev_max_p_kernel(
         for h in range(2):
             multiply(5 + h, 1, 0, h, h + 1)
         multiply(7, 1, 2)
-        nc.vector.tensor_copy(stage[:, :H].rearrange("p (c a) -> p c a", a=PACK), w3_raw[:].rearrange("p a c -> p c a"))
         deal(round_gpsimd, 1, 1, 1, 2)
+        w3_grouped = sb([P, H], BF16, "w3_grouped", "w2_raw")
+        round_gpsimd(w3_grouped[:].rearrange("p (c a) -> p c a", a=PACK), w3_raw[:].rearrange("p a c -> p c a"))
         empty("vector", 1, 0, 0, 1)
         multiply(5, 0, 2)
         empty("vector", 1, 0, 1, 2)
         scatter_scalar(0, 1, (1,))
         scatter_vector(1, 0, 0)
-        settle(0, ["w3", (1, 1)])
+        settle(1, [(1, 1)])
         settle(2, [(1, 3), (0, 3)])
-        w3_codes, w3_scales = quantised["w3"]
         for bank, key in enumerate(((1, 1), (1, 3), (0, 3))):
             multiply(bank, *key)
         scatter_scalar(1, 0, (1,))
@@ -216,7 +216,7 @@ def tile_picked_bev_max_p_kernel(
             nc.vector.tensor_tensor(slot(n, r0, r1), cells(maps[0, n], r0, r1), cells(maps[1, n], r0, r1), MAX)
 
         halves = ((0, S // 2), (S // 2, S))
-        gap = sb([P, S], F32, "gap")
+        gap = sb([P, S], F32, "gap", "w3_raw")
         for r0, r1 in halves:
             nc.gpsimd.tensor_tensor(gap[:, r0:r1], maps[1, 0][:, r0:r1], maps[0, 0][:, r0:r1], SUBTRACT)
         for r0, r1 in halves:
@@ -229,7 +229,7 @@ def tile_picked_bev_max_p_kernel(
         late = sb([P, 2 * V], F32, "late", "stage")
         empty("vector", 1, 2, 0, 2, late[:, :V])
         empty("vector", 1, 1)
-        scatter_vector(1, 1)
+        scatter_vector(1, 2)
         for h in range(2):
             empty("scalar", 0, 2, h, h + 1, late[:, V + h * HALF : V + (h + 1) * HALF])
         scatter_scalar(0, 2, (0,))
@@ -240,11 +240,14 @@ def tile_picked_bev_max_p_kernel(
         cut_piece = sb([P, CUT], F32, "cut_piece")
         nc.scalar.activation(cut_piece[:], accs[0, 3, 0, 2][:, :CUT], RELU)
         scatter_scalar(1, 3, (1,))
-        scatter_vector(1, 2)
+        scatter_vector(1, 1)
         nc.vector.tensor_copy(maps[0, 3][:].indirect(near_sb[:, : CUT // 16]), cut_piece[:])
-        last_piece = sb([P, S], F32, "last_piece", "map0")[:, : V - CUT]
+        last_piece = placed([P, V - CUT], F32, "last_piece", 4 * H)[:]
         nc.scalar.activation(last_piece, accs[0, 3, 0, 2][:, CUT:], RELU)
         nc.scalar.activation(maps[0, 3][:].indirect(near_sb[:, CUT // 16 :]), last_piece, COPY)
+        w3_codes = placed([P, N], U32, "w3_codes", 8 * H)[:].bitcast(FP8X4)
+        w3_scales = sb([P, N], U8, "w3_scales")[:]
+        nc.vector.quantize_mx(out=w3_codes, scales=w3_scales, in_=w3_grouped[:])
         join(1)
         join(2)
 

@@ -23,12 +23,11 @@ LARGEST = 3.4028234663852886e38
 
 P = 128
 PACK = 4
-BLOCK = 128
+RUN = 4
 HALF = V // 2
 AHEAD = 512
-CUT = 160
 PLANE = (0, 2, 1, 3)
-SLOT = (0, 2, 3, 1)
+SLOT = (2, 1, 0, 3)
 CHUNKS = (128, 256, 256, 256, 128)
 MAXIMA = (128, 256, 256, 384)
 
@@ -73,11 +72,17 @@ def tile_picked_bev_max_p_kernel(
         for n in range(PACK):
             nc.sync.dma_start(w3_raw[:, SLOT[n], :], w3_rows[PLANE[n]])
 
-        tiles = [placed([P, S], F32, "map0", 4 * H)] + [sb([P, S], F32, "map%d" % b) for b in range(1, 8)]
+        spots = {0: 14 * H, 3: 14 * H + 4 * S}
+        tiles = [
+            placed([P, S], F32, "map%d" % b, spots[b])
+            if b in spots
+            else sb([P, 2 * S if b // 2 == 2 else S], F32, "map%d" % b)
+            for b in range(8)
+        ]
         for b in range(2):
             nc.vector.memset(tiles[b][:], 0.0)
         for b in range(2, 6):
-            nc.scalar.copy(tiles[b][:], tiles[0][:])
+            nc.scalar.copy(tiles[b][:, :S], tiles[0][:])
         for b in range(6, 8):
             nc.gpsimd.tensor_scalar(tiles[b][:], tiles[1][:], 1.0, 0.0, MULT, ADD)
         maps = {(sensor, n): tiles[2 * n + sensor] for sensor in range(2) for n in range(PACK)}
@@ -93,21 +98,24 @@ def tile_picked_bev_max_p_kernel(
         words = {divmod(g, 2): early[:, g * HALF : (g + 1) * HALF] for g in range(3)}
 
         lead = placed([P, 2 * H], BF16, "lead", 0)
-        stage = sb([P, 4 * H], BF16, "stage")
 
         def round_gpsimd(dst, src):
             nc.gpsimd.tensor_scalar(dst, src, 1.0, 0.0, MULT, ADD)
 
-        def deal(copy, place, sensor, n, count=1, tile=stage):
+        def deal(copy, place, sensor, n, count=1, tile=None):
             dst = tile[:, place * H : (place + count) * H].rearrange("p (t b r) -> p b t r", t=count, r=32)
             rows = raws[sensor][:].rearrange("p j (b u) -> p b u j", u=32)
-            copy(dst, rows[:, :, 8 * PLANE[n] : 8 * (PLANE[n] + count), :])
+            src = rows[:, :, 8 * PLANE[n] : 8 * (PLANE[n] + count), :]
+            if count == 1:
+                dst = dst.rearrange("p b t (c i j) -> p b (t c) j i", i=RUN, j=PACK)
+                src = src.rearrange("p b (c i) j -> p b c j i", i=RUN)
+            copy(dst, src)
 
         quantised = {}
 
-        def settle(place, keys, tile=stage, tag=None):
+        def settle(place, keys, tile):
             width = len(keys) * P
-            codes = sb([P, width], U32, "codes%d_%d" % (place, len(quantised)), tag)
+            codes = sb([P, width], U32, "codes%d_%d" % (place, len(quantised)))
             scales = sb([P, width], U8, "scales%d_%d" % (place, len(quantised)))
             nc.vector.quantize_mx(
                 out=codes[:].bitcast(FP8X4), scales=scales[:], in_=tile[:, place * H : (place + len(keys)) * H]
@@ -166,98 +174,91 @@ def tile_picked_bev_max_p_kernel(
 
         deal(nc.scalar.copy, 0, 0, 0, 1, lead)
         deal(nc.vector.tensor_copy, 1, 0, 1, 1, lead)
+        rest = placed([P, 2 * H], BF16, "rest", 4 * H)
+        deal(nc.vector.tensor_copy, 0, 0, 2, 1, rest)
         settle(0, [(0, 0), (0, 1)], lead)
         for h in range(2):
             for n in range(2):
                 multiply(2 * h + n, 0, n, h, h + 1)
-        deal(nc.scalar.copy, 3, 0, 3)
+        deal(nc.scalar.copy, 1, 0, 3, 1, rest)
         words[1, 1] = pick(placed([P, HALF], U32, "last_words", 0), S - HALF, S)[:]
+        settle(0, [(0, 2), (0, 3)], rest)
         empty("scalar", 0, 0, 0, 1)
         empty("scalar", 0, 1, 0, 1)
         empty("vector", 0, 0, 1, 2)
-        third = placed([P, H], BF16, "third", 2 * H)
-        deal(round_gpsimd, 0, 0, 2, 1, third)
-        deal(round_gpsimd, 0, 1, 0, 2)
+        stage = placed([P, 3 * H], BF16, "stage", 4 * H)
+        deal(round_gpsimd, 0, 1, 0, 2, stage)
         scatter_scalar(0, 0, (0,))
         scatter_vector(0, 1, 0)
         empty("scalar", 0, 1, 1, 2)
         scatter_scalar(0, 0, (1,))
-        settle(0, [(1, 0)])
-        settle(1, [(1, 2)])
-        settle(0, [(0, 2)], third, "res0_0_0")
+        settle(0, [(1, 0)], stage)
+        settle(1, [(1, 2)], stage)
         for h in range(2):
             multiply(5 + h, 1, 0, h, h + 1)
         multiply(7, 1, 2)
-        deal(round_gpsimd, 1, 1, 1, 2)
+        deal(round_gpsimd, 1, 1, 1, 2, stage)
         w3_grouped = sb([P, H], BF16, "w3_grouped", "w2_raw")
         round_gpsimd(w3_grouped[:].rearrange("p (c a) -> p c a", a=PACK), w3_raw[:].rearrange("p a c -> p c a"))
         empty("vector", 1, 0, 0, 1)
         multiply(5, 0, 2)
         empty("vector", 1, 0, 1, 2)
         scatter_scalar(0, 1, (1,))
+        nc.sync.dma_start(maps[0, 2][:, S:], maps[0, 1][:])
         scatter_vector(1, 0, 0)
-        settle(1, [(1, 1)])
-        settle(2, [(1, 3), (0, 3)])
-        for bank, key in enumerate(((1, 1), (1, 3), (0, 3))):
+        settle(1, [(1, 1), (1, 3)], stage)
+        for bank, key in enumerate(((1, 1), (1, 3))):
             multiply(bank, *key)
         scatter_scalar(1, 0, (1,))
 
         pairs = sb([P, PACK * S], BF16, "pairs")
-        pair_view = pairs[:].rearrange("p (b h r e) -> p b h r e", h=2, r=BLOCK, e=2)
-        excess_view = pairs[:].bitcast(F32).rearrange("p (b h r) -> p b h r", h=2, r=BLOCK)
-
-        def cells(tile, r0, r1):
-            return tile[:, r0:r1].rearrange("p (b r) -> p b r", r=BLOCK)
+        pair_view = pairs[:].rearrange("p (h r e) -> p h r e", h=2, e=2)
+        excess = pairs[:].bitcast(F32)
 
         def slot(n, r0, r1):
-            return pair_view[:, r0 // BLOCK : r1 // BLOCK, SLOT[n] // 2, :, SLOT[n] % 2]
-
-        def join(n, r0=0, r1=S):
-            nc.vector.tensor_tensor(slot(n, r0, r1), cells(maps[0, n], r0, r1), cells(maps[1, n], r0, r1), MAX)
+            return pair_view[:, SLOT[n] // 2, r0:r1, SLOT[n] % 2]
 
         halves = ((0, S // 2), (S // 2, S))
         gap = sb([P, S], F32, "gap", "w3_raw")
         for r0, r1 in halves:
             nc.gpsimd.tensor_tensor(gap[:, r0:r1], maps[1, 0][:, r0:r1], maps[0, 0][:, r0:r1], SUBTRACT)
         for r0, r1 in halves:
-            excess = excess_view[:, r0 // BLOCK : r1 // BLOCK, 1, :]
-            nc.gpsimd.tensor_scalar(excess, cells(gap, r0, r1), LARGEST, 0.0, MIN, MAX)
+            nc.gpsimd.tensor_scalar(excess[:, r0:r1], gap[:, r0:r1], LARGEST, 0.0, MIN, MAX)
         for r0, r1 in halves:
-            excess = excess_view[:, r0 // BLOCK : r1 // BLOCK, 1, :]
-            nc.gpsimd.tensor_tensor(slot(0, r0, r1), excess, cells(maps[0, 0], r0, r1), ADD)
+            nc.gpsimd.tensor_tensor(slot(0, r0, r1), excess[:, r0:r1], maps[0, 0][:, r0:r1], ADD)
 
-        late = sb([P, 2 * V], F32, "late", "stage")
+        late = placed([P, 2 * V], F32, "late", 6 * H)
         empty("vector", 1, 2, 0, 2, late[:, :V])
-        empty("vector", 1, 1)
+        multiply(7, 0, 3)
+        empty("vector", 0, 2, 0, 2, late[:, V:])
         scatter_vector(1, 2)
-        for h in range(2):
-            empty("scalar", 0, 2, h, h + 1, late[:, V + h * HALF : V + (h + 1) * HALF])
-        scatter_scalar(0, 2, (0,))
-        for h in range(2):
-            empty("scalar", 1, 3, h, h + 1)
+        empty("scalar", 1, 1)
+        scatter_scalar(1, 1, (0,))
+        empty("scalar", 0, 3)
+        scatter_scalar(1, 1, (1,))
+        nc.sync.dma_start(maps[1, 2][:, S:], maps[1, 1][:])
+        scatter_scalar(0, 3, (0,))
+        empty("scalar", 1, 3, 0, 1)
         scatter_scalar(1, 3, (0,))
-        scatter_scalar(0, 2, (1,))
-        cut_piece = sb([P, CUT], F32, "cut_piece")
-        nc.scalar.activation(cut_piece[:], accs[0, 3, 0, 2][:, :CUT], RELU)
+        scatter_vector(0, 2)
+        scatter_vector(0, 3, 1)
+        empty("scalar", 1, 3, 1, 2, placed([P, HALF], F32, "last_piece", spots[3] - 2 * HALF)[:])
         scatter_scalar(1, 3, (1,))
-        scatter_vector(1, 1)
-        nc.vector.tensor_copy(maps[0, 3][:].indirect(near_sb[:, : CUT // 16]), cut_piece[:])
-        last_piece = placed([P, V - CUT], F32, "last_piece", 4 * H)[:]
-        nc.scalar.activation(last_piece, accs[0, 3, 0, 2][:, CUT:], RELU)
-        nc.scalar.activation(maps[0, 3][:].indirect(near_sb[:, CUT // 16 :]), last_piece, COPY)
-        w3_codes = placed([P, N], U32, "w3_codes", 8 * H)[:].bitcast(FP8X4)
+        w3_codes = placed([P, N], U32, "w3_codes", 18 * H)[:].bitcast(FP8X4)
         w3_scales = sb([P, N], U8, "w3_scales")[:]
         nc.vector.quantize_mx(out=w3_codes, scales=w3_scales, in_=w3_grouped[:])
-        join(1)
-        join(2)
+        both = [maps[sensor, 2][:].rearrange("p (j c i) -> p c j i", j=2, i=RUN) for sensor in range(2)]
+        nc.vector.tensor_tensor(
+            pairs[:, : 2 * S].rearrange("p (c i j) -> p c j i", j=2, i=RUN), both[0], both[1], MAX
+        )
 
         starts = [sum(CHUNKS[:c]) for c in range(len(CHUNKS))]
         grouped = [sb([P, w, 2], U32, "z_grouped%d" % c) for c, w in enumerate(CHUNKS)]
 
         def weave(c):
             r0, r1 = starts[c], starts[c] + CHUNKS[c]
-            pair_words = pairs[:, PACK * r0 : PACK * r1].bitcast(U32).rearrange("p (b h r) -> p b r h", h=2, r=BLOCK)
-            nc.scalar.copy(grouped[c][:].rearrange("p (b r) h -> p b r h", r=BLOCK), pair_words)
+            pair_words = pairs[:].bitcast(U32).rearrange("p (h r) -> p r h", h=2)
+            nc.scalar.copy(grouped[c][:], pair_words[:, r0:r1, :])
 
         def finish(c):
             w = CHUNKS[c]
@@ -285,7 +286,8 @@ def tile_picked_bev_max_p_kernel(
 
         n_chunks = len(CHUNKS)
         for m in range(len(MAXIMA)):
-            join(3, sum(MAXIMA[:m]), sum(MAXIMA[: m + 1]))
+            r0, r1 = sum(MAXIMA[:m]), sum(MAXIMA[: m + 1])
+            nc.vector.tensor_tensor(slot(3, r0, r1), maps[0, 3][:, r0:r1], maps[1, 3][:, r0:r1], MAX)
         for c in range(n_chunks):
             weave(c)
         outs = [finish(c) for c in range(n_chunks)]

@@ -24,6 +24,7 @@ LARGEST = 3.4028234663852886e38
 P = 128
 PACK = 4
 RUN = 4
+CUT = 352
 HALF = V // 2
 AHEAD = 512
 PLANE = (0, 2, 1, 3)
@@ -72,7 +73,7 @@ def tile_picked_bev_max_p_kernel(
         for n in range(PACK):
             nc.sync.dma_start(w3_raw[:, SLOT[n], :], w3_rows[PLANE[n]])
 
-        spots = {0: 14 * H, 3: 14 * H + 4 * S}
+        spots = {0: 18 * H, 3: 18 * H + 4 * S}
         tiles = [
             placed([P, S], F32, "map%d" % b, spots[b])
             if b in spots
@@ -207,8 +208,7 @@ def tile_picked_bev_max_p_kernel(
         nc.sync.dma_start(maps[0, 2][:, S:], maps[0, 1][:])
         scatter_vector(1, 0, 0)
         settle(1, [(1, 1), (1, 3)], stage)
-        for bank, key in enumerate(((1, 1), (1, 3))):
-            multiply(bank, *key)
+        multiply(0, 1, 1)
         scatter_scalar(1, 0, (1,))
 
         pairs = sb([P, PACK * S], BF16, "pairs")
@@ -227,24 +227,25 @@ def tile_picked_bev_max_p_kernel(
         for r0, r1 in halves:
             nc.gpsimd.tensor_tensor(slot(0, r0, r1), excess[:, r0:r1], maps[0, 0][:, r0:r1], ADD)
 
-        late = placed([P, 2 * V], F32, "late", 6 * H)
+        late = placed([P, 3 * V], F32, "late", 6 * H)
         empty("vector", 1, 2, 0, 2, late[:, :V])
         multiply(7, 0, 3)
-        empty("vector", 0, 2, 0, 2, late[:, V:])
+        empty("vector", 1, 1, 0, 2, late[:, V : 2 * V])
+        multiply(0, 1, 3)
+        empty("vector", 0, 2, 0, 2, late[:, 2 * V :])
         scatter_vector(1, 2)
-        empty("scalar", 1, 1)
         scatter_scalar(1, 1, (0,))
         empty("scalar", 0, 3)
         scatter_scalar(1, 1, (1,))
         nc.sync.dma_start(maps[1, 2][:, S:], maps[1, 1][:])
-        scatter_scalar(0, 3, (0,))
         empty("scalar", 1, 3, 0, 1)
+        nc.scalar.activation(maps[0, 3][:].indirect(near_sb[:, : CUT // 16]), res[0, 3][:, :CUT], COPY)
         scatter_scalar(1, 3, (0,))
         scatter_vector(0, 2)
-        scatter_vector(0, 3, 1)
+        nc.vector.tensor_copy(maps[0, 3][:].indirect(near_sb[:, CUT // 16 :]), res[0, 3][:, CUT:])
         empty("scalar", 1, 3, 1, 2, placed([P, HALF], F32, "last_piece", spots[3] - 2 * HALF)[:])
         scatter_scalar(1, 3, (1,))
-        w3_codes = placed([P, N], U32, "w3_codes", 18 * H)[:].bitcast(FP8X4)
+        w3_codes = placed([P, N], U32, "w3_codes", 22 * H)[:].bitcast(FP8X4)
         w3_scales = sb([P, N], U8, "w3_scales")[:]
         nc.vector.quantize_mx(out=w3_codes, scales=w3_scales, in_=w3_grouped[:])
         both = [maps[sensor, 2][:].rearrange("p (j c i) -> p c j i", j=2, i=RUN) for sensor in range(2)]

@@ -24,7 +24,7 @@ LARGEST = 3.4028234663852886e38
 P = 128
 PACK = 4
 RUN = 4
-CUT = 352
+CUT = 320
 HALF = V // 2
 AHEAD = 512
 PLANE = (0, 2, 1, 3)
@@ -182,8 +182,8 @@ def tile_picked_bev_max_p_kernel(
             for n in range(2):
                 multiply(2 * h + n, 0, n, h, h + 1)
         deal(nc.scalar.copy, 1, 0, 3, 1, rest)
-        words[1, 1] = pick(placed([P, HALF], U32, "last_words", 0), S - HALF, S)[:]
         settle(0, [(0, 2), (0, 3)], rest)
+        words[1, 1] = pick(sb([P, HALF], U32, "last_words", "w1_raw"), S - HALF, S)[:]
         empty("scalar", 0, 0, 0, 1)
         empty("scalar", 0, 1, 0, 1)
         empty("vector", 0, 0, 1, 2)
@@ -199,8 +199,6 @@ def tile_picked_bev_max_p_kernel(
             multiply(5 + h, 1, 0, h, h + 1)
         multiply(7, 1, 2)
         deal(round_gpsimd, 1, 1, 1, 2, stage)
-        w3_grouped = sb([P, H], BF16, "w3_grouped", "w2_raw")
-        round_gpsimd(w3_grouped[:].rearrange("p (c a) -> p c a", a=PACK), w3_raw[:].rearrange("p a c -> p c a"))
         empty("vector", 1, 0, 0, 1)
         multiply(5, 0, 2)
         empty("vector", 1, 0, 1, 2)
@@ -210,6 +208,8 @@ def tile_picked_bev_max_p_kernel(
         settle(1, [(1, 1), (1, 3)], stage)
         multiply(0, 1, 1)
         scatter_scalar(1, 0, (1,))
+        w3_grouped = placed([P, H], BF16, "w3_grouped", 4 * H)
+        round_gpsimd(w3_grouped[:].rearrange("p (c a) -> p c a", a=PACK), w3_raw[:].rearrange("p a c -> p c a"))
 
         pairs = sb([P, PACK * S], BF16, "pairs")
         pair_view = pairs[:].rearrange("p (h r e) -> p h r e", h=2, e=2)

@@ -80,12 +80,12 @@ def tile_picked_bev_max_p_kernel(
             else sb([P, 2 * S if b // 2 == 2 else S], F32, "map%d" % b)
             for b in range(8)
         ]
-        for b in range(2):
-            nc.vector.memset(tiles[b][:], 0.0)
-        for b in range(2, 6):
-            nc.scalar.copy(tiles[b][:, :S], tiles[0][:])
-        for b in range(6, 8):
-            nc.gpsimd.tensor_scalar(tiles[b][:], tiles[1][:], 1.0, 0.0, MULT, ADD)
+        zeros = sb([P, 16], F32, "zeros")
+        nc.vector.memset(zeros[:], 0.0)
+        spread = zeros[:].unsqueeze(1).to_broadcast([P, S // 16, 16])
+        for b in range(8):
+            copy = nc.scalar.copy if 2 <= b < 6 else nc.vector.tensor_copy
+            copy(tiles[b][:, :S].rearrange("p (a c) -> p a c", c=16), spread)
         maps = {(sensor, n): tiles[2 * n + sensor] for sensor in range(2) for n in range(PACK)}
 
         picked_scales = sb([P, S], U8, "picked_scales")

@@ -26,7 +26,6 @@ PACK = 4
 RUN = 4
 CUT = 320
 HALF = V // 2
-AHEAD = 512
 PLANE = (0, 2, 1, 3)
 SLOT = (2, 1, 0, 3)
 CHUNKS = (128, 256, 256, 256, 128)
@@ -59,21 +58,22 @@ def tile_picked_bev_max_p_kernel(
         nc.vector.memset(store_scales[:].bitcast(I32), 0)
         nc.sync.dma_start(offs_sb[:], offs)
         words_in = x_words[0].rearrange("p c r -> p (c r)").bitcast(I32)
-        nc.sync.dma_start(store_words[:, :AHEAD], words_in[:, :AHEAD])
+        rows = [w.rearrange("(p j) c -> p j c", j=PACK) for w in (w1, w2)]
+        nc.sync.dma_start(raws[0][:, :1, :], rows[0][:, :1, :])
         nc.sync.dma_start(near_sb[:], near)
         for q in range(4):
             nc.sync.dma_start(
                 store_scales[32 * q : 32 * q + 4, :].bitcast(I32), x_scales[0, 4 * q : 4 * q + 4, :].bitcast(I32)
             )
-        nc.sync.dma_start(store_words[:, AHEAD:], words_in[:, AHEAD:])
-        for raw, w in zip(raws, (w1, w2)):
-            nc.sync.dma_start(raw[:], w.rearrange("(p j) c -> p j c", j=PACK))
+        nc.sync.dma_start(raws[0][:, 1:, :], rows[0][:, 1:, :])
+        nc.sync.dma_start(store_words[:], words_in)
+        nc.sync.dma_start(raws[1][:], rows[1])
         nc.sync.dma_start(far_sb[:], far)
         w3_rows = w3.rearrange("(b t s) c -> t b s c", t=PACK, s=8)
         for n in range(PACK):
             nc.sync.dma_start(w3_raw[:, SLOT[n], :], w3_rows[PLANE[n]])
 
-        spots = {0: 18 * H, 3: 18 * H + 4 * S}
+        spots = {0: 26 * H, 3: 26 * H + 4 * S}
         tiles = [
             placed([P, S], F32, "map%d" % b, spots[b])
             if b in spots
@@ -84,8 +84,13 @@ def tile_picked_bev_max_p_kernel(
         nc.vector.memset(zeros[:], 0.0)
         spread = zeros[:].unsqueeze(1).to_broadcast([P, S // 16, 16])
         for b in range(8):
-            copy = nc.scalar.copy if 2 <= b < 6 else nc.vector.tensor_copy
-            copy(tiles[b][:, :S].rearrange("p (a c) -> p a c", c=16), spread)
+            view = tiles[b][:, :S].rearrange("p (a c) -> p a c", c=16)
+            if b < 4:
+                nc.vector.tensor_copy(view, spread)
+            elif b < 6:
+                nc.scalar.copy(view, spread)
+            else:
+                nc.gpsimd.tensor_scalar(tiles[b][:], tiles[3][:], 1.0, 0.0, MULT, ADD)
         maps = {(sensor, n): tiles[2 * n + sensor] for sensor in range(2) for n in range(PACK)}
 
         picked_scales = sb([P, S], U8, "picked_scales")
@@ -95,9 +100,7 @@ def tile_picked_bev_max_p_kernel(
             nc.vector.tensor_copy(picked[:], store_words[:].bitcast(U32).indirect(offs_sb[:, c0 // 16 : c1 // 16]))
             return picked
 
-        early = pick(sb([P, S - HALF], U32, "early_words"), 0, S - HALF)
-        words = {divmod(g, 2): early[:, g * HALF : (g + 1) * HALF] for g in range(3)}
-
+        words = {}
         lead = placed([P, 2 * H], BF16, "lead", 0)
 
         def round_gpsimd(dst, src):
@@ -129,9 +132,9 @@ def tile_picked_bev_max_p_kernel(
         def multiply(bank, sensor, n, h0=0, h1=2):
             acc = psum.tile([P, (h1 - h0) * HALF], F32, name="acc", tag="bank%d" % bank)
             codes, scales = quantised[sensor, n]
-            runs = [(h0, h1)] if sensor == 0 else [(h, h + 1) for h in range(h0, h1)]
+            runs = [(h0, h1)] if sensor == 1 else [(h, h + 1) for h in range(h0, h1)]
             for a, b in runs:
-                moving = early[:, a * HALF : b * HALF] if sensor == 0 else words[1, a]
+                moving = words[1][:, a * HALF : b * HALF] if sensor == 1 else words[0, a][:]
                 nc.tensor.matmul_mx(
                     out=acc[:, (a - h0) * HALF : (b - h0) * HALF],
                     lhsT=codes,
@@ -177,20 +180,21 @@ def tile_picked_bev_max_p_kernel(
         deal(nc.vector.tensor_copy, 1, 0, 1, 1, lead)
         rest = placed([P, 2 * H], BF16, "rest", 4 * H)
         deal(nc.vector.tensor_copy, 0, 0, 2, 1, rest)
+        deal(nc.scalar.copy, 1, 0, 3, 1, rest)
         settle(0, [(0, 0), (0, 1)], lead)
+        settle(0, [(0, 2), (0, 3)], rest)
         for h in range(2):
+            words[0, h] = pick(sb([P, HALF], U32, "words0_%d" % h), h * HALF, (h + 1) * HALF)
             for n in range(2):
                 multiply(2 * h + n, 0, n, h, h + 1)
-        deal(nc.scalar.copy, 1, 0, 3, 1, rest)
-        settle(0, [(0, 2), (0, 3)], rest)
-        words[1, 1] = pick(sb([P, HALF], U32, "last_words", "w1_raw"), S - HALF, S)[:]
+        words[1] = pick(sb([P, V], U32, "words1"), V, S)
         empty("scalar", 0, 0, 0, 1)
         empty("scalar", 0, 1, 0, 1)
-        empty("vector", 0, 0, 1, 2)
         stage = placed([P, 3 * H], BF16, "stage", 4 * H)
         deal(round_gpsimd, 0, 1, 0, 2, stage)
         scatter_scalar(0, 0, (0,))
         scatter_vector(0, 1, 0)
+        empty("scalar", 0, 0, 1, 2)
         empty("scalar", 0, 1, 1, 2)
         scatter_scalar(0, 0, (1,))
         settle(0, [(1, 0)], stage)
@@ -245,7 +249,7 @@ def tile_picked_bev_max_p_kernel(
         nc.vector.tensor_copy(maps[0, 3][:].indirect(near_sb[:, CUT // 16 :]), res[0, 3][:, CUT:])
         empty("scalar", 1, 3, 1, 2, placed([P, HALF], F32, "last_piece", spots[3] - 2 * HALF)[:])
         scatter_scalar(1, 3, (1,))
-        w3_codes = placed([P, N], U32, "w3_codes", 22 * H)[:].bitcast(FP8X4)
+        w3_codes = placed([P, N], U32, "w3_codes", 30 * H)[:].bitcast(FP8X4)
         w3_scales = sb([P, N], U8, "w3_scales")[:]
         nc.vector.quantize_mx(out=w3_codes, scales=w3_scales, in_=w3_grouped[:])
         both = [maps[sensor, 2][:].rearrange("p (j c i) -> p c j i", j=2, i=RUN) for sensor in range(2)]

from contextlib import ExitStack

import concourse.mybir as mybir

K, T, S, H, N, V = 512, 2048, 1024, 512, 128, 512
FLOPS = 2 * K * H * S + 2 * H * N * S

F32 = mybir.dt.float32
BF16 = mybir.dt.bfloat16
I32 = mybir.dt.int32
U32 = mybir.dt.uint32
U16 = mybir.dt.uint16
U8 = mybir.dt.uint8
FP8X4 = mybir.dt.float8_e4m3fn_x4
RELU = mybir.ActivationFunctionType.Relu
COPY = mybir.ActivationFunctionType.Copy
MAX = mybir.AluOpType.max
MIN = mybir.AluOpType.min
ADD = mybir.AluOpType.add
MULT = mybir.AluOpType.mult
SUBTRACT = mybir.AluOpType.subtract
LARGEST = 3.4028234663852886e38

P = 128
PACK = 4
RUN = 4
CUT = 320
HALF = V // 2
PLANE = (0, 2, 1, 3)
SLOT = (2, 1, 0, 3)
CHUNKS = (128, 256, 256, 256, 128)
MAXIMA = (128, 256, 256, 384)


def tile_picked_bev_max_p_kernel(
    tc, x_words, x_scales, w1, w2, w3, offs, near, far, out
):
    nc = tc.nc
    with ExitStack() as ctx:
        keep = ctx.enter_context(tc.tile_pool(name="keep", bufs=1))
        reuse = ctx.enter_context(tc.tile_pool(name="reuse", bufs=1))
        psum = ctx.enter_context(tc.psum_pool(name="psum", bufs=1))

        def sb(shape, dtype, name, tag=None):
            return keep.tile(shape, dtype, name=name, tag=tag or name, align_bytes=64)

        def placed(shape, dtype, name, offset):
            return reuse.tile(shape, dtype, name=name, offset=offset, align_bytes=64)

        offs_sb = sb([P, S // 16], U16, "offs_sb")
        near_sb = sb([P, V // 16], U16, "near_sb")
        far_sb = sb([P, V // 16], U16, "far_sb")
        store_scales = sb([P, T], U8, "store_scales")
        store_words = sb([P, T], I32, "store_words")
        raws = [sb([P, PACK, H], F32, "w%d_raw" % (s + 1)) for s in range(2)]
        w3_raw = sb([P, PACK, N], F32, "w3_raw")

        nc.vector.memset(store_scales[:].bitcast(I32), 0)
        nc.sync.dma_start(offs_sb[:], offs)
        words_in = x_words[0].rearrange("p c r -> p (c r)").bitcast(I32)
        rows = [w.rearrange("(p j) c -> p j c", j=PACK) for w in (w1, w2)]
        nc.sync.dma_start(raws[0][:, :1, :], rows[0][:, :1, :])
        nc.sync.dma_start(near_sb[:], near)
        for q in range(4):
            nc.sync.dma_start(
                store_scales[32 * q : 32 * q + 4, :].bitcast(I32), x_scales[0, 4 * q : 4 * q + 4, :].bitcast(I32)
            )
        nc.sync.dma_start(raws[0][:, 1:, :], rows[0][:, 1:, :])
        nc.sync.dma_start(store_words[:], words_in)
        nc.sync.dma_start(raws[1][:], rows[1])
        nc.sync.dma_start(far_sb[:], far)
        w3_rows = w3.rearrange("(b t s) c -> t b s c", t=PACK, s=8)
        for n in range(PACK):
            nc.sync.dma_start(w3_raw[:, SLOT[n], :], w3_rows[PLANE[n]])

        spots = {0: 26 * H, 3: 26 * H + 4 * S}
        tiles = [
            placed([P, S], F32, "map%d" % b, spots[b])
            if b in spots
            else sb([P, 2 * S if b // 2 == 2 else S], F32, "map%d" % b)
            for b in range(8)
        ]
        zeros = sb([P, 16], F32, "zeros")
        nc.vector.memset(zeros[:], 0.0)
        spread = zeros[:].unsqueeze(1).to_broadcast([P, S // 16, 16])
        for b in range(8):
            view = tiles[b][:, :S].rearrange("p (a c) -> p a c", c=16)
            if b < 4:
                nc.vector.tensor_copy(view, spread)
            elif b < 6:
                nc.scalar.copy(view, spread)
            else:
                nc.gpsimd.tensor_scalar(tiles[b][:], tiles[3][:], 1.0, 0.0, MULT, ADD)
        maps = {(sensor, n): tiles[2 * n + sensor] for sensor in range(2) for n in range(PACK)}

        picked_scales = sb([P, S], U8, "picked_scales")
        nc.vector.tensor_copy(picked_scales[:], store_scales[:].indirect(offs_sb[:]))

        def pick(picked, c0, c1):
            nc.vector.tensor_copy(picked[:], store_words[:].bitcast(U32).indirect(offs_sb[:, c0 // 16 : c1 // 16]))
            return picked

        words = {}
        lead = placed([P, 2 * H], BF16, "lead", 0)

        def round_gpsimd(dst, src):
            nc.gpsimd.tensor_scalar(dst, src, 1.0, 0.0, MULT, ADD)

        def deal(copy, place, sensor, n, count=1, tile=None):
            dst = tile[:, place * H : (place + count) * H].rearrange("p (t b r) -> p b t r", t=count, r=32)
            rows = raws[sensor][:].rearrange("p j (b u) -> p b u j", u=32)
            src = rows[:, :, 8 * PLANE[n] : 8 * (PLANE[n] + count), :]
            if count == 1:
                dst = dst.rearrange("p b t (c i j) -> p b (t c) j i", i=RUN, j=PACK)
                src = src.rearrange("p b (c i) j -> p b c j i", i=RUN)
            copy(dst, src)

        quantised = {}

        def settle(place, keys, tile):
            width = len(keys) * P
            codes = sb([P, width], U32, "codes%d_%d" % (place, len(quantised)))
            scales = sb([P, width], U8, "scales%d_%d" % (place, len(quantised)))
            nc.vector.quantize_mx(
                out=codes[:].bitcast(FP8X4), scales=scales[:], in_=tile[:, place * H : (place + len(keys)) * H]
            )
            for i, key in enumerate(keys):
                quantised[key] = (codes[:, i * P : (i + 1) * P].bitcast(FP8X4), scales[:, i * P : (i + 1) * P])

        accs = {}

        def multiply(bank, sensor, n, h0=0, h1=2):
            acc = psum.tile([P, (h1 - h0) * HALF], F32, name="acc", tag="bank%d" % bank)
            codes, scales = quantised[sensor, n]
            runs = [(h0, h1)] if sensor == 1 else [(h, h + 1) for h in range(h0, h1)]
            for a, b in runs:
                moving = words[1][:, a * HALF : b * HALF] if sensor == 1 else words[0, a][:]
                nc.tensor.matmul_mx(
                    out=acc[:, (a - h0) * HALF : (b - h0) * HALF],
                    lhsT=codes,
                    lhsT_scale=scales,
                    rhs=moving.bitcast(FP8X4),
                    rhs_scale=picked_scales[:, sensor * V + a * HALF : sensor * V + b * HALF],
                    start=True,
                    stop=True,
                )
            accs[sensor, n, h0, h1] = acc[:]
            for h in range(h0, h1):
                accs[sensor, n, h, h + 1] = acc[:, (h - h0) * HALF : (h - h0 + 1) * HALF]

        lists = (near_sb, far_sb)
        res = {}

        def empty(engine, sensor, n, h0=0, h1=2, tile=None):
            if tile is None:
                tile = sb([P, (h1 - h0) * HALF], F32, "res%d_%d_%d" % (sensor, n, h0))[:]
            src = accs[sensor, n, h0, h1]
            if engine == "scalar":
                nc.scalar.activation(tile, src, RELU)
            else:
                nc.vector.tensor_scalar_max(tile, src, 0.0)
            for h in range(h0, h1):
                res[sensor, n, h] = tile[:, (h - h0) * HALF : (h - h0 + 1) * HALF]
            res[sensor, n] = tile

        def window(sensor, n, h0, h1):
            return maps[sensor, n][:].indirect(lists[sensor][:, h0 * HALF // 16 : h1 * HALF // 16])

        def scatter_scalar(sensor, n, halves=(0, 1)):
            for h in halves:
                nc.scalar.activation(window(sensor, n, h, h + 1), res[sensor, n, h], COPY)

        def scatter_vector(sensor, n, h=None):
            if h is None:
                nc.vector.tensor_copy(window(sensor, n, 0, 2), res[sensor, n])
            else:
                nc.vector.tensor_copy(window(sensor, n, h, h + 1), res[sensor, n, h])

        deal(nc.scalar.copy, 0, 0, 0, 1, lead)
        deal(nc.vector.tensor_copy, 1, 0, 1, 1, lead)
        rest = placed([P, 2 * H], BF16, "rest", 4 * H)
        deal(nc.vector.tensor_copy, 0, 0, 2, 1, rest)
        deal(nc.scalar.copy, 1, 0, 3, 1, rest)
        settle(0, [(0, 0), (0, 1)], lead)
        settle(0, [(0, 2), (0, 3)], rest)
        for h in range(2):
            words[0, h] = pick(sb([P, HALF], U32, "words0_%d" % h), h * HALF, (h + 1) * HALF)
            for n in range(2):
                multiply(2 * h + n, 0, n, h, h + 1)
        words[1] = pick(sb([P, V], U32, "words1"), V, S)
        empty("scalar", 0, 0, 0, 1)
        empty("scalar", 0, 1, 0, 1)
        stage = placed([P, 3 * H], BF16, "stage", 4 * H)
        deal(round_gpsimd, 0, 1, 0, 2, stage)
        scatter_scalar(0, 0, (0,))
        scatter_vector(0, 1, 0)
        empty("scalar", 0, 0, 1, 2)
        empty("scalar", 0, 1, 1, 2)
        scatter_scalar(0, 0, (1,))
        settle(0, [(1, 0)], stage)
        settle(1, [(1, 2)], stage)
        for h in range(2):
            multiply(5 + h, 1, 0, h, h + 1)
        multiply(7, 1, 2)
        deal(round_gpsimd, 1, 1, 1, 2, stage)
        empty("vector", 1, 0, 0, 1)
        multiply(5, 0, 2)
        empty("vector", 1, 0, 1, 2)
        scatter_scalar(0, 1, (1,))
        nc.sync.dma_start(maps[0, 2][:, S:], maps[0, 1][:])
        scatter_vector(1, 0, 0)
        settle(1, [(1, 1), (1, 3)], stage)
        multiply(0, 1, 1)
        scatter_scalar(1, 0, (1,))
        w3_grouped = placed([P, H], BF16, "w3_grouped", 4 * H)
        round_gpsimd(w3_grouped[:].rearrange("p (c a) -> p c a", a=PACK), w3_raw[:].rearrange("p a c -> p c a"))

        pairs = sb([P, PACK * S], BF16, "pairs")
        pair_view = pairs[:].rearrange("p (h r e) -> p h r e", h=2, e=2)
        excess = pairs[:].bitcast(F32)

        def slot(n, r0, r1):
            return pair_view[:, SLOT[n] // 2, r0:r1, SLOT[n] % 2]

        halves = ((0, S // 2), (S // 2, S))
        gap = sb([P, S], F32, "gap", "w3_raw")
        for r0, r1 in halves:
            nc.gpsimd.tensor_tensor(gap[:, r0:r1], maps[1, 0][:, r0:r1], maps[0, 0][:, r0:r1], SUBTRACT)
        for r0, r1 in halves:
            nc.gpsimd.tensor_scalar(excess[:, r0:r1], gap[:, r0:r1], LARGEST, 0.0, MIN, MAX)
        for r0, r1 in halves:
            nc.gpsimd.tensor_tensor(slot(0, r0, r1), excess[:, r0:r1], maps[0, 0][:, r0:r1], ADD)

        late = placed([P, 3 * V], F32, "late", 6 * H)
        empty("vector", 1, 2, 0, 2, late[:, :V])
        multiply(7, 0, 3)
        empty("vector", 1, 1, 0, 2, late[:, V : 2 * V])
        multiply(0, 1, 3)
        empty("vector", 0, 2, 0, 2, late[:, 2 * V :])
        scatter_vector(1, 2)
        scatter_scalar(1, 1, (0,))
        empty("scalar", 0, 3)
        scatter_scalar(1, 1, (1,))
        nc.sync.dma_start(maps[1, 2][:, S:], maps[1, 1][:])
        empty("scalar", 1, 3, 0, 1)
        nc.scalar.activation(maps[0, 3][:].indirect(near_sb[:, : CUT // 16]), res[0, 3][:, :CUT], COPY)
        scatter_scalar(1, 3, (0,))
        scatter_vector(0, 2)
        nc.vector.tensor_copy(maps[0, 3][:].indirect(near_sb[:, CUT // 16 :]), res[0, 3][:, CUT:])
        empty("scalar", 1, 3, 1, 2, placed([P, HALF], F32, "last_piece", spots[3] - 2 * HALF)[:])
        scatter_scalar(1, 3, (1,))
        w3_codes = placed([P, N], U32, "w3_codes", 30 * H)[:].bitcast(FP8X4)
        w3_scales = sb([P, N], U8, "w3_scales")[:]
        nc.vector.quantize_mx(out=w3_codes, scales=w3_scales, in_=w3_grouped[:])
        both = [maps[sensor, 2][:].rearrange("p (j c i) -> p c j i", j=2, i=RUN) for sensor in range(2)]
        nc.vector.tensor_tensor(
            pairs[:, : 2 * S].rearrange("p (c i j) -> p c j i", j=2, i=RUN), both[0], both[1], MAX
        )

        starts = [sum(CHUNKS[:c]) for c in range(len(CHUNKS))]
        grouped = [sb([P, w, 2], U32, "z_grouped%d" % c) for c, w in enumerate(CHUNKS)]

        def weave(c):
            r0, r1 = starts[c], starts[c] + CHUNKS[c]
            pair_words = pairs[:].bitcast(U32).rearrange("p (h r) -> p r h", h=2)
            nc.scalar.copy(grouped[c][:], pair_words[:, r0:r1, :])

        def finish(c):
            w = CHUNKS[c]
            codes = sb([P, w], U32, "z%d_codes" % c)
            scales = sb([P, w], U8, "z%d_scales" % c)
            flat = grouped[c][:].rearrange("p r h -> p (r h)").bitcast(BF16)
            nc.vector.quantize_mx(out=codes[:].bitcast(FP8X4), scales=scales[:], in_=flat)
            acc = psum.tile([P, w], F32, name="acc_out", tag="bank%d" % (3 + c))
            nc.tensor.matmul_mx(
                out=acc[:],
                lhsT=w3_codes,
                lhsT_scale=w3_scales,
                rhs=codes[:].bitcast(FP8X4),
                rhs_scale=scales[:],
                start=True,
                stop=True,
            )
            return acc

        def store(c, acc, copy):
            w = CHUNKS[c]
            staged = sb([P, w], F32, "staged%d" % c)
            copy(staged[:], acc[:])
            nc.sync.dma_start(out[:, starts[c] : starts[c] + w], staged[:])

        n_chunks = len(CHUNKS)
        for m in range(len(MAXIMA)):
            r0, r1 = sum(MAXIMA[:m]), sum(MAXIMA[: m + 1])
            nc.vector.tensor_tensor(slot(3, r0, r1), maps[0, 3][:, r0:r1], maps[1, 3][:, r0:r1], MAX)
        for c in range(n_chunks):
            weave(c)
        outs = [finish(c) for c in range(n_chunks)]
        for c in range(n_chunks):
            store(c, outs[c], nc.vector.tensor_copy if c >= n_chunks - 1 else nc.scalar.copy)
